import numpy as np, ml_dtypes
CORES = [25,29,65,69,153,157,193,197]
N = 8
import mx_ref
BF = ml_dtypes.bfloat16
def gentries(a):
    return np.ascontiguousarray(a.reshape(8, 16, -1).transpose(0, 2, 1)).reshape(8, -1)
def gtable(e):
    e = np.asarray(e); return np.ascontiguousarray(e.reshape(8, -1, 16).transpose(0, 2, 1)).reshape(128, -1).astype(np.int32)
def gcols(t, e):
    v = np.concatenate([t.reshape(8, 16, -1, 4), np.zeros((8, 16, 1, 4), BF)], axis=2)
    return np.ascontiguousarray(np.stack([v[g][:, e[g]] for g in range(8)])).reshape(128, -1)
def tile(rs):
    return np.stack(rs, axis=2).reshape(128, -1).astype(BF)
def pick(q, e):
    c = np.concatenate([q[0].reshape(128, -1, 4), np.zeros((128, 1, 4), np.uint8)], axis=1); s = np.concatenate([q[1], np.ones((16, 1), np.uint8)], axis=1)
    return (np.ascontiguousarray(c[:, e].reshape(128, -1)), np.ascontiguousarray(s[:, e]))
def join(*qs):
    return (np.concatenate([q[0] for q in qs], axis=1), np.concatenate([q[1] for q in qs], axis=1))
def put(q, e, v):
    c, s = q[0].reshape(128, -1, 4).copy(), q[1].copy(); c[:, e] = v[0].reshape(128, -1, 4); s[:, e] = v[1]
    return (c.reshape(128, -1), s)
def pk(c, s):
    return (np.ascontiguousarray(c), mx_ref.live(s))
def emit(q):
    return q[0], q[1]
def packed(v, rng):
    q = [mx_ref.quantize(np.ascontiguousarray(v[r])) for r in range(N)]
    return np.stack([a for a, b in q]), np.stack([mx_ref.plane(b, rng) for a, b in q])
def values_of_codes():
    e, c = np.zeros((128, 128, 4), np.float32), np.zeros((128, 2, 4), np.uint8)
    e[np.arange(128), np.arange(128), 0] = 1
    c[:127, :, 0] = np.arange(256).reshape(2, 128).T[:127]
    return mx_ref.matmul(mx_ref.quantize(e.reshape(128, 512).astype(BF)), (c.reshape(128, 8), np.full((16, 2), 127, np.uint8))).T.reshape(-1).astype(np.float64)
CODE_VALUE, SCALE_VALUE = values_of_codes(), 2.0 ** (np.arange(256) - 127.0)
def decode(q):
    return (CODE_VALUE[q[0]].reshape(16, 8, -1, 4) * SCALE_VALUE[q[1]][:, None, :, None] + 0.0).reshape(128, -1).astype(np.float32)
def f(rng, *shape):
    return mx_ref.flush((rng.standard_normal(shape, dtype=np.float32) * np.exp2(rng.integers(-2, 3, shape[:-1] + (1,)))).astype(BF))
def wide(rng, *shape, cols=0):
    v = rng.standard_normal(shape, dtype=np.float32) * np.exp2(rng.integers(-12, 13, shape)).astype(np.float32)
    if cols: v *= np.repeat(np.exp2(rng.integers(-cols, cols + 1, shape[:-2] + (1, shape[-1] // 4))) * (rng.random(shape[:-2] + (1, shape[-1] // 4)) > 0.0625), 4, axis=-1).astype(np.float32)
    return mx_ref.flush(v.astype(BF))
C = 288
TURN = [1, 2, 4]
def numbers_of(rng):
    return {"x": np.array(f(rng, N, 128, 4 * C)), "u": np.array(f(rng, N, 128, 512)), "v": np.array(f(rng, N, 128, 512))}
def rotors(rng):
    return np.argsort(rng.random((N, 8, C)), axis=2)
def stored(e):
    return np.stack([gtable(e[r]) for r in range(N)])
def layers(rng):
    return 2.0 * rng.random((N, 128, 4, 128, 4)) - 1.0
def kept(rng):
    w, i = layers(rng), np.arange(16)
    w[:, :, :, :16] = 0
    for b in range(4): w[:, i, b, i, b] = 1
    return w
def weights(rng, w):
    c, s = packed(np.ascontiguousarray(w).reshape(N, 128, 2048).astype(np.float32).astype(BF), rng)
    return {"wc": c, "ws": s}
def setup_inputs(rng):
    return {**numbers_of(rng), "p": stored(rotors(rng)), **weights(rng, layers(rng))}
def setup_inputs_ties(rng):
    d = numbers_of(rng)
    o = rng.permutation(N)
    k = rng.integers(-2, 3, (N, C))
    k[o[0]] = 1
    k[o[1]] = 0
    k[o[2]] = -1 - rng.integers(0, 2, C)
    x = d["x"].reshape(N, 128, C, 4)
    x[:, :16] = 0
    x[:, 0, :, 0] = k.astype(np.float32).astype(BF)
    u = d["u"].reshape(N, 128, 128, 4)
    u[:, :, 0] = 0
    u[:, :, 1::16] = 0
    for r in range(N):
        u[r, 0, 0, 0] = 1.0 if o[r] % 2 == 0 else -1.0
        u[r, 0, 1::16, 0] = rng.permutation([1, 1, 1, -1, -1, -1, 0, 0]).astype(np.float32).astype(BF)
    return {"x": x.reshape(N, 128, 4 * C), "u": u.reshape(N, 128, 512), "v": d["v"], "p": stored(rotors(rng)), **weights(rng, kept(rng))}
def setup_inputs_near(rng):
    d = numbers_of(rng)
    s = rng.integers(0, 16, (N, C))
    size = np.where(np.arange(N) // 2 % 2 == rng.integers(2), 2.0 ** 9, 2.0 ** -7)[:, None]
    x = d["x"].astype(np.float32).reshape(N, 128, C, 4)
    x[:, :16] = 0
    x[:, 0, :, 0] = rng.integers(-1, 2, (N, C)) * size
    x[:, 8] = ((s[:, :, None] >> np.arange(4)) & 1) * np.exp2(np.arange(4) - 23.0) * size[:, :, None]
    x[:, 11, :, 0] = 2.0 ** -10 * size
    u = d["u"].reshape(N, 128, 128, 4)
    u[:, :, 0] = 0
    u[:, :, 1::16] = 0
    w = kept(rng)
    odd = int(rng.integers(2))
    for r in range(N):
        k = 1.0 if r % 2 == odd else 2.0 ** -30
        if r % 2 != odd: w[r, :, :, :16] *= 0.0625
        u[r, 0, 0, 0] = k
        u[r, 8, 0] = k
        u[r, 11, 0, 0] = k
        h = rng.permutation(8)
        for g in range(8):
            if h[g] < 4: u[r, 8, 16 * g + 1] = k
            else: u[r, 0, 16 * g + 1, 0] = -k
    return {"x": x.reshape(N, 128, 4 * C).astype(BF), "u": u.reshape(N, 128, 512), "v": d["v"], "p": stored(rotors(rng)), **weights(rng, w)}
def setup_inputs_huge(rng):
    d = numbers_of(rng)
    o = rng.permutation(N)
    e = rotors(rng)
    e[o < N // 2, 1:] = np.arange(C)
    x = 2.0 ** 25 * (0.75 + 0.25 * rng.random((N, 128, C, 4)))
    x[o == 0] = 2.0 ** 25
    u = d["u"].reshape(N, 128, 128, 4)
    for r in range(N):
        k = rng.permutation(C)
        t = 1.0 - 0.125 * (k // 2 % 2)
        t = t * (k % 2 * 2.0 - 1.0) if o[r] < N // 2 else t * (o[r] % 2 * 2.0 - 1.0)
        x[r] *= t[None, :, None]
        u[r, :, 0] = ((rng.integers(2) * 2.0 - 1.0) * 2.0 ** 30 * (1.0 - 0.1 * rng.random((128, 4)))).astype(np.float32).astype(BF)
        u[r, :, 1::16] = ((rng.permutation(8) % 2 * 2.0 - 1.0)[None, :, None] * 2.0 ** 30 * (1.0 - 0.1 * rng.random((128, 8, 4)))).astype(np.float32).astype(BF)
    return {"x": x.astype(np.float32).reshape(N, 128, 4 * C).astype(BF), "u": u.reshape(N, 128, 512), "v": d["v"], "p": stored(e), **weights(rng, np.ones((N, 128, 4, 128, 4)))}
def setup_inputs_ends(rng):
    d = numbers_of(rng)
    o = rng.permutation(N)
    e = rotors(rng)
    i = np.arange(C)
    x = np.full((N, 128, C, 4), 2.0 ** 25)
    w = np.ones((N, 128, 4, 128, 4))
    u = d["u"].reshape(N, 128, 128, 4)
    for r in range(N):
        k = o[r] % 4
        if k == 0:
            e[r, 1:] = i
            x[r, :, rng.integers(C)] *= -1.0
        elif k == 2: e[r] = (i + C - 1) % C
        else:
            if k == 1: e[r] = i[::-1]
            x[r, 32:] *= rng.integers(0, 2, (96, C, 4)) * 2.0 - 1.0
            x[r, 64:] *= 2.0 ** -55
        x[r] *= rng.integers(2) * 2.0 - 1.0
        a = 2.0 ** -30 if o[r] == 1 else 2.0 ** 30
        u[r, :, 0] = a * (rng.integers(2) * 2.0 - 1.0)
        t = rng.permutation([1, 1, 1, 1, -1, -1, -1, 0]) * a
        u[r, :, 1::16] = t.astype(np.float32).astype(BF)[None, :, None]
        if o[r] == 3: w[r, 64:] = (rng.integers(0, 2, (64, 4, 128, 4)) * 2.0 - 1.0) * 2.0 ** -30
    d["v"] = (np.where(d["v"] < 0, -1.0, 1.0) * np.where(rng.permutation(N) % 2, 2.0 ** -30, 2.0 ** 30)[:, None, None]).astype(np.float32).astype(BF)
    return {"x": x.astype(np.float32).reshape(N, 128, 4 * C).astype(BF), "u": u.reshape(N, 128, 512), "v": d["v"], "p": stored(e), **weights(rng, w)}
def setup_inputs_spread(rng):
    d = setup_inputs(rng)
    d["x"] = wide(rng, N, 128, 4 * C, cols=6)
    return d
def check_inputs(d):
    b = []
    for k, top in (("x", 2.0 ** 25), ("u", 2.0 ** 30), ("v", 2.0 ** 30)):
        a = np.abs(d[k].astype(np.float32))
        if not (np.isfinite(a).all() and ((a == 0) | (a >= 2.0 ** -30) & (a <= top)).all()): b.append("a value of " + k)
    none, least, most = [emit(mx_ref.quantize(np.full((128, 16), k, np.float32).astype(BF)))[1][0, 0] for k in (0.0, 2.0 ** -30, 1.0)]
    for r in range(N):
        if (np.sort(gentries(d["p"][r]), axis=1) != np.arange(C)).any(): b.append("p: a group without a permutation")
        if ((d["wc"][r] & 0x7F) == 0x7F).any(): b.append("wc: a code that is no number")
        s = mx_ref.live(d["ws"][r])
        if ((s != none) & ((s < least) | (s > most))).any(): b.append("ws: a scale out of range")
        elif (np.abs(decode(pk(d["wc"][r], d["ws"][r]))) > 1).any(): b.append("a number of W beyond 1")
    return b
def reference(x, u, v, p, wc, ws):
    qu = [mx_ref.quantize(u[r]) for r in range(N)]
    lay = [pk(wc[r], ws[r]) for r in range(N)]
    rho = np.stack([gentries(p[r]) for r in range(N)])
    now = [x[r] for r in range(N)]
    a = np.zeros((N, 8), np.int64)
    op = np.zeros((N, 8, C), np.float32)
    for h in TURN:
        e = np.zeros((N, 8, C), np.int64)
        j = np.zeros((N, 1), np.int64) + np.arange(C)
        for g in range(8):
            j = (np.take_along_axis(rho[:, g], (j + a[:, g:g + 1]) % C, axis=1) - a[:, g:g + 1]) % C
            e[:, g] = j
        back = np.argsort(e, axis=2)
        for r in range(N):
            b = r ^ h
            part = gcols(now[r], e[r])
            q = mx_ref.quantize(part)
            z = mx_ref.quantize(tile([mx_ref.matmul(pick(lay[b], np.arange(128 * k, 128 * k + 128)), q) * np.float32(0.0078125) for k in range(4)]))
            s = mx_ref.matmul(qu[b], z) + np.float32(0.0)
            o = np.argsort(-s[0], kind="stable")
            m = np.zeros(C, np.int64)
            m[o[::2]] = o[1::2]
            m[o[1::2]] = o[::2]
            mixed = ((part.astype(np.float32) + decode(z)) * np.float32(0.5)).astype(BF)
            come = m[back[r]]
            now[r] = gcols(mixed, come)
            a[r] = (a[r] + np.sum(s[1::16] > 0, axis=1)) % C
            op[r] = (np.take_along_axis(e[r], come, axis=1) + a[r][:, None]) % C
    y = np.zeros((N, 128, C), np.float32)
    oc, osc = np.zeros((N, 128, 4 * C), np.uint8), np.zeros((N, 16, C), np.uint8)
    for r in range(N):
        q = mx_ref.quantize(now[r])
        y[r] = mx_ref.matmul(mx_ref.quantize(v[r]), q)
        oc[r], osc[r] = emit(q)
    return {"y": y, "op": op, "oc": oc, "osc": osc}

@@ -1,0 +1,581 @@
+from concourse.mybir import dt, AluOpType, ActivationFunctionType
+
+C = 288
+NB = 96
+TURN = [1, 2, 4]
+MID = 144.0
+MAGIC = 12582912.0
+TINY = 2.0 ** -110
+BATCH = False
+LIFT = 3.0 * C - MID
+SPLIT = 32
+HALVES = True
+PIECES = [(0, 32), (32, 72)]
+WHO = ["vs", "vs", "vs", "vs"]
+CR = "v"
+TAILS = False
+FILL = "sss"
+EVAC = ["sssvsssv", "ssssssss", "svsvsvsv"]
+
+X4, U8 = "float8_e4m3fn_x4", "uint8"
+
+SCRATCH = {"ps": ("psum", [128, 4096], "float32")}
+for _n, _w in (("wl", 512), ("w1", 512), ("w2", 512), ("w3", 512), ("rw", 512), ("qu", 128), ("us", 128), ("u1", 128),
+               ("u2", 128), ("u3", 128), ("ru", 128), ("qv", 128), ("qe", 512), ("qo", 256), ("qf", C), ("qh", 320),
+               ("qn", 136), ("qm", C), ("qx", C)):
+    SCRATCH[_n + "c"] = ("sbuf", [128, _w], X4)
+    SCRATCH[_n + "s"] = ("sbuf", [128, _w], U8)
+for _n, _w in (("xin", 4 * C), ("uin", 512), ("vin", 512), ("ft", 4 * C), ("ht", 4 * C), ("et", 2048), ("ot", 1024),
+               ("nt", 544), ("mt", 4 * C), ("zt", 576), ("sg", C), ("thr", C), ("st", 4 * C)):
+    SCRATCH[_n] = ("sbuf", [128, _w], "bfloat16")
+for _n in ("iot", "ca", "cb", "cc", "cd", "era", "erb", "ei", "wr", "d16", "d4", "order", "mr", "cr"):
+    SCRATCH[_n] = ("sbuf", [128, C], "bfloat16")
+for _n in ("sc2", "sc3", "sc4"):
+    SCRATCH[_n] = ("sbuf", [128, C], "float16")
+for _n in ("tab", "lx", "lt", "ly"):
+    SCRATCH[_n] = ("sbuf", [128, 176], "float16")
+SCRATCH["lq"] = ("sbuf", [128, 176], "bfloat16")
+for _n, _w in (("mod", 4 * C), ("sc", C), ("psm", 144), ("ea", C), ("opr", C), ("yt", C), ("idn", 176), ("idm", 176), ("sm", 32), ("sm1", 32), ("sm2", 32), ("sm3", 32), ("last", 32), ("dp", 32),
+               ("col", 16), ("tiny", 8), ("kk", 32), ("wa", 32), ("wb", 32), ("scol", 8), ("ia", 16), ("ib", 16),
+               ("ic", 16), ("ie", 16), ("acol", 16)):
+    SCRATCH[_n] = ("sbuf", [128, _w], "float32")
+for _n, _w in (("pt", 176), ("pi", 8), ("pj", 8), ("pk", 8)):
+    SCRATCH[_n] = ("sbuf", [128, _w], "int32")
+for _n, _w in (("ls", 176), ("e16", 18), ("w16", 18), ("r16", 18), ("h16", 18), ("c4", 72), ("ul", 8),
+               ("ml", 18), ("ix", 12), ("k16", 18), ("a16", 18)):
+    SCRATCH[_n] = ("sbuf", [128, _w], "uint16")
+
+SEMAPHORES = (["qv", "qs", "qt", "qg", "sent", "aw1a", "aw1b", "aw1s", "au1", "aw2", "aw3", "ar0", "ar1", "ar2"]
+              + ["d%d" % _k for _k in range(40)])
+
+A = AluOpType
+F = ActivationFunctionType
+WAKE = 70.0
+
+
+def relays_of(src, far, T, topo):
+    return [c for c in topo.cores_of(src)
+            if T.rank_of(c) is None and topo.die(c) == topo.die(src) and all(topo.may_write(c, d) for d in far)][:2]
+
+
+def count(mask):
+    return bin(mask).count("1")
+
+
+def depend(ops):
+    wr, rd, groups = {}, {}, {}
+    for i, o in enumerate(ops):
+        if o["kind"] == "dma":
+            groups.setdefault(o["grp"] or "x%d" % i, []).append(i)
+    for name, members in groups.items():
+        for j in members:
+            ops[j]["grp"] = name
+    for i, o in enumerate(ops):
+        deps = set()
+        for k in o["r"]:
+            if k in wr:
+                deps.add(wr[k])
+            if k.startswith("ps") and k != "psm":
+                deps.update(j for j in rd.get(k, []) if ops[j]["q"] != o["q"])
+        for k in o["w"]:
+            if k in wr:
+                deps.add(wr[k])
+            deps.update(rd.get(k, []))
+        for j in list(deps):
+            if ops[j]["kind"] == "dma":
+                deps.update(groups[ops[j]["grp"]])
+        o["deps"] = sorted(j for j in deps if ops[j]["kind"] != "remote")
+        for k in o["r"]:
+            rd.setdefault(k, []).append(i)
+        for k in o["w"]:
+            wr[k] = i
+            rd[k] = []
+    return groups
+
+
+def arrange(ops):
+    n = len(ops)
+    level = [o["lat"] for o in ops]
+    after = [o["deps"] + o.get("like", []) for o in ops]
+    for i in range(n - 1, -1, -1):
+        level[i] += ops[i]["tail"]
+        for j in after[i]:
+            level[j] = max(level[j], ops[j]["lat"] + WAKE + level[i])
+    busy = {q: [] for q in "vstgy"}
+    start, end = [0.0] * n, [0.0] * n
+    for i in sorted(range(n), key=lambda i: (-level[i], i)):
+        o = ops[i]
+        t = max([o["at"]] + [end[j] + (1.0 if o["q"] == "t" and ops[j]["q"] == "t" else WAKE) for j in after[i]])
+        if o["kind"] != "arrive":
+            for a, b in sorted(busy[o["q"]]):
+                if t + o["c"] <= a:
+                    break
+                t = max(t, b)
+            busy[o["q"]].append((t, t + o["c"]))
+        start[i], end[i] = t, t + o["lat"]
+    return sorted(range(n), key=lambda i: (start[i], i))
+
+
+def emit(g, T, ops):
+    eng = {"v": g.vector, "s": g.scalar, "t": g.tensor, "g": g, "y": g.sync}
+    groups = depend(ops)
+    order = ORDER if len(ORDER) == len(ops) else arrange(ops)
+    known = {q: {} for q in eng}
+    pos = {q: 0 for q in eng}
+    for i in order:
+        o = ops[i]
+        q = o["q"]
+        best = {}
+        for j in o["deps"]:
+            p = ops[j]
+            if p["q"] == "t" and q == "t":
+                continue
+            a, b = p["id"]
+            if known[q].get(a, -1) < b and (a not in best or ops[best[a]]["id"][1] < b):
+                best[a] = j
+        waits = []
+        for j in sorted(best.values(), key=lambda j: -len(ops[j]["clock"])):
+            p = ops[j]
+            if known[q].get(p["id"][0], -1) >= p["id"][1]:
+                continue
+            waits.append(j)
+            p["need"] = True
+            for a, b in list(p["clock"].items()) + [p["id"]]:
+                if known[q].get(a, -1) < b:
+                    known[q][a] = b
+        o["waits"] = waits
+        o["clock"] = dict(known[q]) if o["kind"] != "arrive" else {}
+        if o["kind"] == "op":
+            o["id"] = (q, pos[q])
+            pos[q] += 1
+        else:
+            o["id"] = (o["grp"] or "x%d" % i, 0)
+    for n, members in enumerate(groups.values()):
+        for j in members:
+            ops[j]["sem"], ops[j]["val"] = T.sem["d%d" % n], 16 * len(members)
+    cnt = {q: 0 for q in eng}
+    for i in order:
+        o = ops[i]
+        q = o["q"]
+        for j in o["waits"]:
+            eng[q].wait_ge(ops[j]["sem"], ops[j]["val"])
+        if o["kind"] == "arrive":
+            continue
+        ins = o["fn"](eng[q])
+        if o["kind"] == "dma":
+            ins.then_inc(o["sem"], 16)
+        elif o["kind"] == "op" and o.get("need"):
+            cnt[q] += 1
+            o["sem"], o["val"] = T.sem["q" + q], cnt[q]
+            ins.then_inc(o["sem"], 1)
+    for members in groups.values():
+        if not any(ops[j].get("need") for j in members):
+            o = ops[members[-1]]
+            eng[o["q"]].wait_ge(o["sem"], o["val"])
+
+
+RELAYED = [[("w", "s", 0, 512), ("w", "c", 0, 256)], [("w", "c", 256, 512), ("u", "c", 0, 128), ("u", "s", 0, 128)]]
+
+
+def relay_program(g, core, src, far, which, T, topo):
+    n = count(topo.mask(src, core))
+    total = 0
+    for i in range(2):
+        rid, pid = topo.addr(far[i], core)
+        m = topo.mask(core, far[i])
+        for k, (name, kind, a, b) in enumerate(RELAYED[which]):
+            if i == 0:
+                g.wait_ge(T.sem["ar%d" % k], n)
+            out, in_ = T["%s%d%s" % (name, i + 2, kind)][:, a:b], T["r" + name + kind][:, a:b]
+            if kind == "c":
+                out, in_ = out.bitcast(dt.uint8), in_.bitcast(dt.uint8)
+            g.remote_dma(out, in_, T.sem["aw%d" % (i + 2)], T.sem.sent, pid, rid, m)
+            total += count(m)
+    g.wait_ge(T.sem.sent, total)
+
+
+def rank_program(g, core, T, topo):
+    rank = T.rank_of(core)
+    cores = list(T.cores)
+    if rank is None:
+        for r, c in enumerate(cores):
+            far = [cores[r ^ h] for h in TURN[1:]]
+            for which, d in enumerate(relays_of(c, far, T, topo)):
+                if d == core:
+                    relay_program(g, core, c, far, which, T, topo)
+        return
+
+    ops = []
+
+    def op(q, r, w, fn, c, kind="op", grp=None, lat=None, at=0.0, tail=0.0):
+        ops.append({"q": q, "r": r, "w": w, "fn": fn, "kind": kind, "grp": grp, "c": c, "lat": lat or c, "at": at, "tail": tail})
+
+    def el(n):
+        return 25.0 + max(64.0, n)
+
+    def dma(q, r, w, out, in_, lat, grp=None, at=0.0, **kw):
+        op(q, r, w, lambda e: e.dma_start(out, in_, **kw), 60.0, "dma", grp, lat, at)
+
+    def arrive(w, sem, val, like):
+        op("g", [], w, None, 1.0, "arrive")
+        ops[-1].update(sem=sem, val=val, like=like)
+
+    sent = [0]
+
+    def send(r, dst, out, in_, sem, lat):
+        rid, pid = topo.addr(dst, core)
+        m = topo.mask(core, dst)
+        op("g", r, [], lambda e: e.remote_dma(out, in_, sem, T.sem.sent, pid, rid, m), 150.0 if sent[0] else 1600.0, "remote", lat=lat)
+        sent[0] += count(m)
+        return len(ops) - 1
+
+    def u8(name, a, b):
+        return T[name][:, a:b].bitcast(dt.uint8)
+
+    def bank(b, a=0, n=C, p=128, step=1):
+        return T.ps[0:p, 512 * b + a:512 * b + a + n:step]
+
+    def memset(w, ap, v, n=0):
+        op("v", [], w, lambda e: e.memset(ap, v), el(n))
+
+    def ts(r, w, out, in0, s1, o0, s2=None, o1=None, n=0):
+        if o1 is None:
+            op("v", r, w, lambda e: e.tensor_scalar(out, in0, s1, None, o0), el(n))
+        else:
+            op("v", r, w, lambda e: e.tensor_scalar(out, in0, s1, s2, o0, o1), el(n))
+
+    def tt(r, w, out, in0, in1, o, n=0):
+        op("v", r, w, lambda e: e.tensor_tensor(out, in0, in1, o), el(n))
+
+    def cp(r, w, out, in_, n=0):
+        op("v", r, w, lambda e: e.tensor_copy(out, in_), el(n))
+
+    def act(r, w, out, in_, func, n=0, **kw):
+        op("s", r, w, lambda e: e.activation(out, in_, func, **kw), el(n) + 10.0)
+
+    def move(q, r, w, out, in_, n, scale=None):
+        if q == "s":
+            if scale is None:
+                act(r, w, out, in_, F.Copy, n)
+            else:
+                act(r, w, out, in_, F.Copy, n, scale=scale)
+        elif scale is None:
+            cp(r, w, out, in_, n)
+        else:
+            ts(r, w, out, in_, scale, A.mult, n=n)
+
+    def quant(r, name, a, b, in_, w=None):
+        op("v", r, w or [name], lambda e: e.quantize_mx(T[name + "c"][:, a:b], T[name + "s"][:, a:b], in_), 15.0 + 1.1 * (b - a))
+
+    def mm(r, b, n, l, la, m, ma, start=True, stop=True):
+        op("t", r, ["ps%d" % b], lambda e: e.matmul_mx(bank(b, 0, n), T[l + "c"][:, la:la + 128], T[l + "s"][:, la:la + 128],
+                                                      T[m + "c"][:, ma:ma + n], T[m + "s"][:, ma:ma + n], start, stop),
+           0.63 * (n + 16))
+
+    def gather(q, win, lst, out, a=0, off=0, width=C, r=()):
+        move(q, [win, lst] + list(r), [out], T[out][:, 0:C], T[win][:, a:a + width].indirect(T[lst][:, off:off + 18]), 400)
+
+    def scatter(src, lst, out):
+        cp([src, lst], [out], T[out][:, 0:C].indirect(T[lst][:]), T[src][:, 0:C], 930)
+
+    def scan(r, src, pat, out, n=150):
+        op("v", r + [pat], [out], lambda e: e.tensor_tensor_scan(T[out][:], src, T[pat][:], -2.0 * C, A.max, A.add), el(n))
+
+    def wrap16(row, lst, via):
+        scan([row], T[row][:], "d16", via)
+        ts([via], [lst], T[lst][:], T[via][:, 15:C:16], C + MID, A.add)
+
+    tails = [(0, 4 * SPLIT), (4 * SPLIT, C)] if TAILS else [(0, C)]
+
+    def part_gather(q, rw, win, rl, lst, off, out, i, a, b):
+        move(q, rw + rl, ["%s%d" % (out, i)], T[out][:, a:b], T[win][:].indirect(T[lst][:, off + a // 16:off + b // 16]), 30 + 1.3 * (b - a))
+
+    def part_scan(row, pat, out, i, a, b):
+        op("v", ["%s%d" % (row, i), pat], ["%s%d" % (out, i)],
+           lambda e: e.tensor_tensor_scan(T[out][:, a:b], T[row][:, a:b], T[pat][:, a:b], -2.0 * C, A.max, A.add), el((b - a) / 2))
+
+    def part_wrap4(row, i, a, b):
+        part_scan(row, "d4", "sc4", i, a, b)
+        ts(["sc4%d" % i, "col2"], ["c4%d" % i], T.c4[:, a // 4:b // 4], T.sc4[:, a + 3:b:4], 4.0, A.mult, T.col[:, 2:3], A.add)
+
+    def iota(w, out, pattern, base, cm, n, small=True):
+        if small:
+            op("g", [], w, lambda e: e.iota(out, pattern, base, cm, allow_small_or_imprecise_dtypes=True), 160.0 + 2.1 * n)
+        else:
+            op("g", [], w, lambda e: e.iota(out, pattern, base, cm), 160.0 + 2.1 * n)
+
+    def select(r, w, out, in_, pattern, cmp, fill, base, cm, n):
+        op("g", r, w, lambda e: e.affine_select(out, in_, pattern, cmp, fill, base, cm), 210.0 + 2.1 * n)
+
+    helpers = [cores[rank ^ h] for h in TURN]
+
+    pts = ["pt%d" % s for s in range(8)]
+    memset(["pt"], T.pt[:], 0, 176)
+    for s in range(8):
+        dma("ys"[s % 2], ["pt"], [pts[s]], T.pt[16 * s:128, 18 * s:18 * s + 18], T.p[0:128 - 16 * s, :], 2300.0, "p")
+    dma("y", [], ["wls"], T.wls[:], T.ws[:], 2200.0)
+    dma("y", [], ["wla"], u8("wlc", 0, 256), T.wc[:, 0:1024], 2900.0, at=600.0)
+    dma("y", [], ["wlb"], u8("wlc", 256, 512), T.wc[:, 1024:2048], 3400.0, at=670.0)
+    dma("y", [], ["uin"], T.uin[:], T.u[:], 3900.0, at=740.0)
+    dma("y", [], ["xin"], T.xin[:], T.x[:], 5000.0, at=810.0)
+
+    iota(["pi"], T.pi[:, 0:1], [[0, 1]], 0, 1, 1, False)
+    iota(["sm"], T.sm[:, 0:16], [[1, 16]], 0, 0, 16)
+    iota(["smb"], T.sm[:, 16:32], [[0, 4], [1, 4]], 0, 0, 16)
+    iota(["idn"], T.idn[:, 0:162], [[0, 9], [16, 18]], 0, 0, 162)
+    iota(["iot"], T.iot[:], [[1, C]], -int(MID), 0, C)
+    iota(["pk"], T.pk[:, 0:2], [[-112, 2]], 112, 8, 2, False)
+    ts(["pi"], ["pj0"], T.pj[:, 0:1], T.pi[:, 0:1], 15, A.bitwise_and)
+    ts(["pi"], ["pj1"], T.pj[:, 1:2], T.pi[:, 0:1], 2, A.arith_shift_right, 3, A.bitwise_and)
+    ts(["pi"], ["pj2"], T.pj[:, 2:3], T.pi[:, 0:1], 3, A.bitwise_and)
+    ts(["pi"], ["pj3"], T.pj[:, 3:4], T.pi[:, 0:1], 4, A.arith_shift_right)
+    cp(["pj0", "pj1", "pj2", "pj3"], ["col", "col2"], T.col[:, 0:4], T.pj[:, 0:4])
+    ts(["col2"], ["col2"], T.col[:, 2:3], T.col[:, 2:3], 4.0 * (C + MID), A.add)
+    memset(["last"], T.last[:], 0.0)
+    memset(["last"], T.last[:, 15:32:4], -2.0 * C)
+    ts(["col", "idn"], ["idn"], T.idn[:, 0:162], T.idn[:, 0:162], T.col[:, 0:1], A.add, LIFT, A.add, n=162)
+    select(["idn"], ["idm"], T.idm[:, 0:162], T.idn[:, 0:162], [[16, 9], [0, 18]], A.is_ge, LIFT, -1, -1, 162)
+    ts(["col", "sm"], ["sm1a"], T.sm1[:, 0:16], T.sm[:, 0:16], T.col[:, 0:1], A.subtract)
+    ts(["col", "smb"], ["sm1b"], T.sm1[:, 16:32], T.sm[:, 16:32], T.col[:, 1:2], A.subtract)
+    ts(["col", "idn"], ["ml"], T.ml[:], T.idn[:, 0:18], 0.0, A.mult, T.col[:, 0:1], A.add)
+    ts(["sm1a", "sm1b"], ["sm2"], T.sm2[:], T.sm1[:], 0.0, A.is_equal, float(C), A.mult)
+    ts(["sm1a", "sm1b"], ["sm3"], T.sm3[:], T.sm1[:], -1.0, A.is_equal, -1024.0, A.mult)
+    tt(["sm2", "last"], ["sm2"], T.sm2[:], T.sm2[:], T.last[:], A.add)
+    tt(["sm2", "sm3"], ["dp"], T.dp[:], T.sm2[:], T.sm3[:], A.add)
+    gather("s", "dp", "ml", "d16", 0, 0, 16)
+    gather("s", "dp", "ml", "d4", 16, 0, 16)
+    memset(["ul0"], T.ul[:, 0:6], 0)
+    ts(["pk"], ["pk"], T.pk[:, 0:2], T.pk[:, 0:2], 127, A.bitwise_and)
+    ts(["pk"], ["ul1"], T.ul[:, 6:8], T.pk[:, 0:2], 1.0, A.add)
+    ts(["last"], ["tabp"], T.tab[:, 162:176], T.last[:, 0:14], LIFT, A.add)
+    memset(["zt"], T.zt[:], 0.0, 290)
+    memset(["ota"], T.ot[:, 0:512], 0.5, 260)
+    act(["ota"], ["otb"], T.ot[:, 512:1024], T.ot[:, 0:512], F.Copy, 520, scale=-1.0)
+    for how, w, out, in_ in zip(FILL, (["mta"], ["mtb"], ["nt0", "nt1", "nt2"]), (T.mt[:, 0:576], T.mt[:, 576:1152], T.nt[:]),
+                                (T.zt[:], T.zt[:], T.zt[:, 0:544])):
+        if how == "s":
+            act(["zt"], w, out, in_, F.Copy, 590)
+        elif how == "v":
+            memset(w, out, 0.0, 290)
+        else:
+            dma("y", ["zt"], w, out, in_, 3000.0)
+    memset(["tiny"], T.tiny[:], -TINY)
+    for b in range(4):
+        select(["ota"], ["et%d" % b], T.et[:, 512 * b:512 * b + 512], T.ot[:, 0:512], [[1, 512]], A.is_equal, 0.0, -b, -4, 512)
+    select(["ota"], ["thr"], T.thr[:], T.ot[:, 0:C], [[0, 3], [-1, NB]], A.is_ge, -0.5, 0, 1, C)
+    quant(["zt"], "qh", 192, 320, T.zt[:, 0:512])
+    quant(["ota", "otb"], "qo", 0, 256, T.ot[:])
+    quant(["et0", "et1"], "qe", 0, 256, T.et[:, 0:1024], ["qe0"])
+    quant(["et2", "et3"], "qe", 256, 512, T.et[:, 1024:2048], ["qe1"])
+    memset(["kk"], T.kk[:], 0.0)
+    memset(["kk"], T.kk[:, 16:24], 144.0)
+    memset(["kk"], T.kk[:, 8:9], 144.0)
+    ts(["idn"], ["ia"], T.ia[:, 0:12], T.idn[:, 0:12], -8.5 - LIFT, A.add, 1.0 / 18.0, A.mult)
+    ts(["ia"], ["ia"], T.ia[:, 0:12], T.ia[:, 0:12], MAGIC, A.add, MAGIC, A.subtract)
+    ts(["ia", "col"], ["ib"], T.ib[:, 0:12], T.ia[:, 0:12], T.col[:, 3:4], A.subtract, 2.0, A.min)
+    ts(["ia"], ["ic"], T.ic[:, 0:12], T.ia[:, 0:12], 0.0, A.is_equal, 7.0, A.mult)
+    ts(["ib"], ["ie"], T.ie[:, 0:12], T.ib[:, 0:12], 2.0, A.is_equal, -7.0, A.mult)
+    tt(["ic", "ib"], ["ic"], T.ic[:, 0:12], T.ic[:, 0:12], T.ib[:, 0:12], A.subtract)
+    tt(["ic", "ie"], ["ic"], T.ic[:, 0:12], T.ic[:, 0:12], T.ie[:, 0:12], A.add)
+    ts(["ic"], ["ix"], T.ix[:], T.ic[:, 0:12], 9.0, A.add)
+    for o in ops:
+        if o["w"] and o["w"][0] in SOON:
+            o["tail"] = SOON[o["w"][0]]
+
+    n1 = count(topo.mask(helpers[0], core))
+    arrive(["w1s"], T.sem.aw1s, n1, [send(["wls"], helpers[0], T.w1s[:], T.wls[:], T.sem.aw1s, 4200.0)])
+    arrive(["w1a"], T.sem.aw1a, n1, [send(["wla"], helpers[0], u8("w1c", 0, 256), u8("wlc", 0, 256), T.sem.aw1a, 3400.0)])
+    arrive(["w1b"], T.sem.aw1b, n1, [send(["wlb"], helpers[0], u8("w1c", 256, 512), u8("wlc", 256, 512), T.sem.aw1b, 3800.0)])
+    quant(["uin"], "qu", 0, 128, T.uin[:])
+    cp(["qu", "ul0", "ul1"], ["usc"], T.usc[:].bitcast(dt.uint32), T.quc[:].bitcast(dt.uint32).indirect(T.ul[:]), 200)
+    act(["qu", "ul0", "ul1"], ["uss"], T.uss[:], T.qus[:].indirect(T.ul[:]), F.Copy, 200)
+    arrive(["u1"], T.sem.au1, 2 * n1, [send(["usc"], helpers[0], u8("u1c", 0, 128), u8("usc", 0, 128), T.sem.au1, 3500.0),
+                                       send(["uss"], helpers[0], T.u1s[:], T.uss[:], T.sem.au1, 3500.0)])
+    to = relays_of(core, helpers[1:], T, topo)
+    like = [send(["wls", "wlb"], to[0], T.rws[:], T.wls[:], T.sem.ar0, 9000.0),
+            send(["wla", "wlb"], to[0], u8("rwc", 0, 256), u8("wlc", 0, 256), T.sem.ar1, 9000.0),
+            send(["wlb"], to[1], u8("rwc", 256, 512), u8("wlc", 256, 512), T.sem.ar0, 9000.0),
+            send(["usc"], to[1], u8("ruc", 0, 128), u8("usc", 0, 128), T.sem.ar1, 9000.0),
+            send(["uss"], to[1], T.rus[:], T.uss[:], T.sem.ar2, 9000.0)]
+    for i in (1, 2):
+        src = relays_of(helpers[i], [cores[rank ^ TURN[i] ^ h] for h in TURN[1:]], T, topo)
+        arrive(["w%d" % (i + 1), "u%d" % (i + 1)], T.sem["aw%d" % (i + 1)],
+               sum(len(RELAYED[k]) * count(topo.mask(src[k], core)) for k in range(2)), like)
+    dma("g", ["usc", "uss"], ["vin"], T.vin[:], T.v[:], 9000.0)
+    ops[-1]["tail"] = 22000.0
+    quant(["vin"], "qv", 0, 128, T.vin[:])
+
+    tt(pts + ["idm"], ["tab"], T.tab[:, 0:162], T.pt[:, 0:162], T.idm[:, 0:162], A.add, 330)
+    ts(["tab"], ["ls", "lsb"], T.ls[:, 0:162], T.tab[:, 0:162], LIFT, A.subtract, n=162)
+    for s in range(NA):
+        gather("s", "iot" if s == 0 else ("cb", "ca")[s % 2], "ls", ("ca", "cb")[s % 2], 0, 18 * s, r=["lsb"])
+    for s in range(8 - NA):
+        gather("v", "iot" if s == 0 else ("cd", "cc")[s % 2], "ls", ("cc", "cd")[s % 2], 0, 18 * (s + NA), r=["lsb"])
+    wrap16(("cc", "cd")[(7 - NA) % 2], "w16", "sc2")
+    gather("s", ("ca", "cb")[(NA - 1) % 2], "w16", "era")
+    ops[-1]["w"] = ["era", "era0", "era1"]
+    ops[-1]["r"] = ops[-1]["r"] + ["w160", "w161"]
+    for i, (a, b) in enumerate(tails):
+        part_wrap4("era", i, a, b)
+
+    def data_gather(win, scale, turn):
+        for i, (a, b) in enumerate(PIECES):
+            q = WHO[turn][i]
+            move(q, ["c4%d" % k for k, (c, d) in enumerate(tails) if c < 4 * b and d > 4 * a] + [win], ["ft%d" % i], T.ft[:, 16 * a:16 * b], T[win][:].indirect(T.c4[:, a:b]), 30 + 21 * (b - a), scale)
+
+    def ft(a, b):
+        return ["ft%d" % i for i, (c, d) in enumerate(PIECES) if 4 * c < b and 4 * d > a]
+
+    def lists(k, a, b):
+        n = b - a
+        tt(["wa", "ix", "tab", "tabp"], ["lx" + k], T.lx[:, a:b], T.wa[:].indirect(T.ix[:, a // 16:b // 16]), T.tab[:, a:b], A.add, 30 + 1.3 * n)
+        ts(["lx" + k], ["lq" + k], T.lq[:, a:b], T.lx[:, a:b], 1.0 / C, A.mult, 128.0 + 0.5 / C, A.add, n=n / 2)
+        ts(["lq" + k], ["lt" + k], T.lt[:, a:b], T.lq[:, a:b], 128.0, A.subtract, -float(C), A.mult, n=n / 2)
+        op("v", ["lx" + k, "lt" + k], ["ly" + k],
+           lambda e: e.tensor_tensor_scan(T.ly[:, a:b], T.lx[:, a:b], T.lt[:, a:b], 0.0, A.max, A.add), el(n / 2))
+        ts(["ly" + k], ["ls", "lsb"] if n == 176 else ["ls" + k], T.ls[:, a:b], T.ly[:, a:b], MID, A.add, n=n / 2)
+
+    def compare(key, t, a, b, o):
+        ts(["ps7", "scol", "mta", "mtb"], [key], T.mt[0:NB, 4 * a + t:4 * b:4], bank(7, a, b - a, NB), T.scol[0:NB, t:t + 1], o, n=b - a)
+
+    sts = ["st0", "st1", "st2", "st3"]
+    e_now, e_new = "era", "erb"
+    parts = [(0, 4 * SPLIT), (4 * SPLIT, C)] if HALVES else [(0, C)]
+    qh = ["qh%d" % i for i in range(len(parts))]
+    for rnd in range(3):
+        wn, un = "w%d" % (rnd + 1), "u%d" % (rnd + 1)
+        wkeys = [["w1s", "w1a"], ["w1s", "w1a"], ["w1s", "w1b"], ["w1s", "w1b"]] if rnd == 0 else [[wn]] * 4
+        data_gather("xin" if rnd == 0 else "st", None if rnd == 0 else 0.5, rnd)
+        wrap16(e_now, "e16", "sc3")
+        if rnd < 2:
+            scatter("iot", "e16", "ei")
+        for i, (a, b) in enumerate(parts):
+            quant(ft(a, b), "qf", a, b, T.ft[:, 4 * a:4 * b], ["qf%d" % i])
+            for k in range(4):
+                mm(["qf%d" % i] + wkeys[k], 4 * i + k, b - a, wn, 128 * k, "qf", a)
+            for k in range(4):
+                move(EVAC[rnd][4 * i + k], ["ps%d" % (4 * i + k)], ["ht%d" % (4 * i + k)], T.ht[:, 4 * a + k:4 * b:4],
+                     bank(4 * i + k, 0, b - a), b - a, 0.0078125)
+            quant(["ht%d" % (4 * i + k) for k in range(4)] + ["qh"], "qh", a, b, T.ht[:, 4 * a:4 * b], ["qh%d" % i])
+        for t in range(3):
+            mm([k for k, (a, b) in zip(qh, parts) if a < NB * t + 128 and b > NB * t] + [un], 4 + t, 128, "qh", NB * t, un, 0)
+        mm(qh + [un], 7, C, un, 0, "qh", 0)
+        mm(qh + [un], 0, C, un, 0, "qh", 0)
+        for b in range(3):
+            mm(qh + ["qe%d" % (b // 2)], 1 + b, C, "qe", 128 * b, "qh", 0)
+        for t in range(3):
+            act(["ps%d" % (4 + t), "tiny"], ["nt%d" % t], T.nt[0:NB, 36 + t:96 + t:4], bank(4 + t, 98, 30, NB, 2), F.Sign,
+                bias=T.tiny[0:NB, 0:1])
+        act(["ps4", "ps5", "ps6"], ["scol"], T.scol[0:NB, 0:3], T.ps[0:NB, 2048:3073:512], F.Copy)
+        quant(["nt0", "nt1", "nt2"], "qn", 0, 136, T.nt[:])
+        mm(["qn", "qo"], 5, 128, "qo", 0, "qn", 8, True, False)
+        mm(["qn", "qo"], 5, 128, "qo", 128, "qn", 0, False, True)
+        mm(qh + ["qe1"], 4, C, "qe", 384, "qh", 0)
+        for t in range(3):
+            act(["ps0", "scol"], ["sg%d" % t], T.sg[0:NB, NB * t:NB * t + NB], bank(0, NB * t, NB, NB), F.Sign, NB,
+                bias=T.scol[0:NB, t:t + 1], scale=-1.0)
+        for b in range(4):
+            act(["ps%d" % (1 + b)] + ft(0, C), [sts[b]], T.st[:, b:4 * C:4], bank(1 + b), F.Copy, 300, scale=2.0)
+        dma("g", sts + ft(0, C), ["st"], T.st[:], T.ft[:], 4000.0, accum_op=A.add)
+        base = "kk" if rnd == 0 else "wb"
+        tt(["ps5", base], ["wa"], T.wa[:], bank(5, 0, 32), T[base][:], A.add)
+        if rnd < 2:
+            if BATCH:
+                lists("", 0, 64)
+                lists("b", 64, 176)
+            else:
+                lists("", 0, 176)
+            tt(["wa", "kk"], ["wb"], T.wb[:], T.wa[:], T.kk[:], A.add)
+            src = "ei"
+            for s in range(8):
+                dst = ("ca", "cb")[s % 2]
+                gather("s", src, "ls", dst, 0, 18 * s, r=["lsb"] if 18 * s + 18 > 64 else [])
+                src = dst
+            for i, (a, b) in enumerate(tails):
+                part_gather("s", [src], src, ["ls", "lsb"], "ls", 18 * 8, "wr", i, a, b)
+                part_scan("wr", "d16", "sc2", i, a, b)
+                ts(["sc2%d" % i], ["w16%d" % i], T.w16[:, a // 16:b // 16], T.sc2[:, a + 15:b:16], C + MID, A.add)
+            gather("s", e_now, "w16", e_new, r=["w16%d" % i for i in range(len(tails))])
+            e_now, e_new = e_new, e_now
+        else:
+            iota(["mod"], T.mod[:], [[0, 4], [1, C]], 0, 0, 4 * C)
+            ops[-1]["r"] = ["thr", "et3", "usc"]
+            cp(["wa", "ix"], ["acol"], T.acol[:], T.wa[:].indirect(T.ix[:, 0:1]))
+            ts(["acol", "e16"], ["a16"], T.a16[:], T.e16[:], T.acol[:, 0:1], A.subtract, 3.0 * C, A.add)
+            gather("s", "mod", "a16", "ea", 0, 0, 4 * C)
+        compare("mt0", 0, NB, C, A.is_le)
+        compare("mt1", 1, 0, NB, A.is_lt)
+        compare("mt2", 1, 2 * NB, C, A.is_le)
+        compare("mt3", 2, 0, 2 * NB, A.is_lt)
+        tt(["sg0", "sg1", "sg2", "thr", "mta", "mtb"], ["mt4"], T.mt[0:NB, 3:4 * C:4], T.sg[0:NB, :], T.thr[0:NB, :], A.is_gt, 590)
+        quant(["mt0", "mt1", "mt2", "mt3", "mt4"], "qm", 0, C, T.mt[:])
+        mm(["qm", "qo"], 6, C, "qo", 0, "qm", 0)
+        scan(["ps6"], bank(6), "d16", "sc", 300)
+        ts(["sc"], ["r16"], T.r16[:], T.sc[:, 15:C:16], float(C), A.add, 2.0, A.mult)
+        ts(["sc"], ["h16"], T.h16[:], T.sc[:, 15:C:16], C - 0.25, A.add)
+        scatter("iot", "r16", "order")
+        tt(["order"], ["psm"], T.psm[:], T.order[:, 0:C:2], T.order[:, 1:C:2], A.add, 300)
+        tt(["psm", "h16", "iot"], ["mr"], T.mr[:], T.psm[:].indirect(T.h16[:]), T.iot[:, 0:C], A.subtract, 400)
+        if rnd == 2:
+            scatter("mr", "e16", "cr")
+            ops[-1]["w"] = ["cr"] + ["cr%d" % i for i in range(len(tails))]
+        for i, (a, b) in enumerate(tails):
+            if rnd < 2:
+                part_gather(CR[i], ["mr"], "mr", ["w16%d" % i], "w16", 0, "cr", i, a, b)
+            part_wrap4("cr", i, a, b)
+
+    data_gather("st", 0.5, 3)
+    a = 4 * SPLIT
+    quant(ft(0, a), "qx", 0, a, T.ft[:, 0:4 * a], ["qxa"])
+    quant(ft(a, C), "qx", a, C, T.ft[:, 4 * a:4 * C], ["qxb"])
+    mm(["qxa", "qv"], 0, a, "qv", 0, "qx", 0)
+    mm(["qxb", "qv"], 7, C - a, "qv", 0, "qx", a)
+    dma("y", ["qxa"], [], T.oc[:, 0:4 * a], u8("qxc", 0, a), 2300.0, "o")
+    dma("y", ["qxb"], [], T.oc[:, 4 * a:4 * C], u8("qxc", a, C), 2300.0, "o")
+    wrap16("cr", "k16", "sc3")
+    move("s", ["ps0"], ["yta"], T.yt[:, 0:a], bank(0, 0, a), a)
+    move("s", ["ps7"], ["ytb"], T.yt[:, a:C], bank(7, 0, C - a), C - a)
+    for k in range(4):
+        dma("y", ["qxa", "qxb"], [], T.osc[4 * k:4 * k + 4, :], T.qxs[32 * k:32 * k + 4, :], 2000.0, "o")
+    dma("s", ["yta"], [], T.y[:, 0:a], T.yt[:, 0:a], 2300.0, "z")
+    dma("s", ["ytb"], [], T.y[:, a:C], T.yt[:, a:C], 2300.0, "z")
+    gather("v", "ea", "k16", "opr")
+    dma("y", ["opr"], [], T.op[:], T.opr[0:128:16, :], 2000.0, "o")
+
+    emit(g, T, ops)
+    g.wait_ge(T.sem.sent, sent[0])
+
+
+NA = 5
+ORDER = [
+    15, 14, 19, 16, 17, 18, 0, 44, 22, 23, 21, 43, 20, 9, 4, 8, 6, 2, 5, 7, 3, 1, 11, 10, 12, 13, 59, 24, 26, 28, 31, 30, 27, 62, 33,
+    34, 60, 32, 35, 63, 36, 29, 70, 74, 50, 72, 84, 71, 45, 48, 64, 65, 66, 91, 61, 92, 37, 38, 67, 25, 49, 98, 39, 40, 99, 68, 100,
+    55, 101, 76, 102, 41, 93, 94, 95, 96, 97, 103, 78, 56, 77, 104, 105, 107, 47, 75, 51, 79, 80, 73, 86, 82, 85, 83, 53, 81, 52, 89,
+    54, 108, 106, 109, 111, 121, 110, 115, 114, 112, 124, 125, 122, 123, 113, 118, 116, 128, 126, 127, 117, 129, 119, 130, 120, 57,
+    42, 69, 46, 133, 132, 131, 141, 140, 139, 142, 143, 58, 136, 135, 144, 145, 137, 138, 146, 134, 150, 147, 149, 148, 151, 153,
+    152, 155, 156, 157, 158, 159, 160, 176, 175, 174, 177, 178, 162, 163, 164, 165, 166, 167, 168, 169, 170, 179, 161, 90, 180, 181,
+    182, 183, 184, 185, 186, 171, 172, 187, 188, 173, 154, 189, 192, 190, 195, 191, 193, 205, 323, 87, 194, 196, 199, 208, 207, 209,
+    197, 206, 198, 200, 203, 212, 211, 213, 210, 202, 201, 214, 204, 217, 216, 215, 225, 224, 223, 226, 227, 220, 218, 222, 228, 229,
+    219, 230, 221, 234, 236, 231, 233, 232, 237, 235, 261, 259, 88, 238, 239, 240, 241, 242, 243, 244, 260, 258, 262, 246, 247, 248,
+    249, 250, 251, 252, 253, 254, 263, 264, 245, 265, 266, 267, 268, 269, 270, 255, 256, 271, 272, 273, 274, 278, 257, 275, 288, 282,
+    281, 280, 289, 292, 279, 290, 291, 286, 284, 296, 285, 294, 293, 283, 287, 295, 297, 276, 298, 300, 299, 301, 302, 306, 309, 307,
+    308, 314, 315, 316, 277, 328, 330, 327, 329, 331, 310, 305, 303, 304, 313, 311, 312, 319, 317, 320, 318, 321, 332, 333, 322, 324,
+    334, 325, 335, 336, 337, 338, 339, 340, 326, 341, 342, 344, 343, 345, 346, 351, 352, 347, 348, 349, 361, 353, 359, 354, 360, 355,
+    357, 358, 362, 356, 350]
+ORDER = [
+    14, 19, 16, 15, 17, 18, 0, 43, 23, 20, 22, 21, 9, 2, 8, 6, 4, 5, 3, 1, 7, 10, 12, 11, 13, 26, 24, 44, 27, 28, 31, 30, 62, 33, 32,
+    25, 35, 34, 63, 40, 36, 64, 29, 39, 66, 41, 91, 59, 70, 72, 51, 74, 84, 71, 47, 48, 45, 37, 38, 92, 65, 98, 49, 67, 93, 94, 95,
+    96, 97, 99, 68, 76, 100, 77, 101, 55, 102, 103, 56, 60, 42, 69, 104, 78, 79, 50, 75, 80, 82, 85, 86, 83, 52, 53, 73, 54, 81, 105,
+    108, 107, 106, 109, 111, 121, 113, 112, 123, 124, 114, 125, 122, 115, 117, 127, 128, 118, 126, 116, 110, 129, 119, 130, 120, 61,
+    57, 46, 133, 132, 131, 141, 140, 139, 142, 143, 58, 135, 136, 144, 145, 137, 138, 134, 146, 147, 149, 148, 150, 151, 152, 153,
+    155, 156, 157, 158, 159, 175, 160, 176, 174, 177, 178, 162, 163, 164, 165, 166, 167, 168, 169, 170, 89, 154, 87, 179, 180, 161,
+    181, 182, 183, 184, 90, 185, 186, 88, 323, 171, 172, 187, 173, 188, 192, 189, 190, 191, 195, 193, 205, 194, 199, 196, 208, 209,
+    197, 206, 207, 198, 203, 200, 212, 213, 210, 211, 201, 202, 214, 204, 217, 215, 216, 225, 223, 224, 226, 220, 218, 222, 227, 228,
+    229, 221, 219, 230, 234, 236, 235, 232, 231, 237, 233, 261, 260, 239, 240, 241, 242, 243, 244, 246, 247, 248, 249, 250, 251, 252,
+    253, 254, 258, 259, 262, 263, 264, 245, 265, 238, 266, 267, 268, 269, 270, 255, 256, 271, 272, 273, 274, 278, 257, 275, 288, 280,
+    281, 282, 284, 289, 290, 286, 294, 279, 292, 296, 291, 285, 293, 283, 295, 287, 297, 298, 299, 300, 301, 302, 306, 307, 309, 308,
+    316, 314, 315, 276, 277, 329, 327, 328, 330, 331, 310, 304, 305, 303, 313, 311, 312, 318, 319, 320, 317, 321, 332, 333, 322, 324,
+    334, 335, 325, 337, 336, 338, 339, 340, 326, 341, 342, 343, 345, 344, 346, 351, 352, 347, 348, 349, 361, 353, 359, 354, 360, 357,
+    356, 355, 362, 358, 350]
+SOON = {"qe0": 5000.0, "qe1": 5000.0, "qo": 2000.0, "ix": 2000.0, "qh": 1000.0, "mta": 4000.0, "mtb": 4000.0, "nt0": 2000.0,
+        "thr": 3000.0, "tiny": 2000.0, "tabp": 2000.0, "d16": 1000.0, "d4": 1000.0}

@@ -3,6 +3,7 @@ from concourse.mybir import dt, AluOpType, ActivationFunctionType
 C = 288
 NB = 96
 TURN = [1, 2, 4]
+WORLD = 256
 MID = 144.0
 MAGIC = 12582912.0
 TINY = 2.0 ** -110
@@ -12,7 +13,10 @@ SPLIT = 32
 HALVES = True
 PIECES = [(0, 32), (32, 72)]
 WHO = ["vs", "vs", "vs", "vs"]
-CR = "v"
+CR = "sv"
+NC = 5
+FOLD = True
+LAST = False
 TAILS = False
 FILL = "sss"
 EVAC = ["sssvsssv", "ssssssss", "svsvsvsv"]
@@ -20,7 +24,7 @@ EVAC = ["sssvsssv", "ssssssss", "svsvsvsv"]
 X4, U8 = "float8_e4m3fn_x4", "uint8"
 
 SCRATCH = {"ps": ("psum", [128, 4096], "float32")}
-for _n, _w in (("wl", 512), ("w1", 512), ("w2", 512), ("w3", 512), ("rw", 512), ("qu", 128), ("us", 128), ("u1", 128),
+for _n, _w in (("wl", 512), ("w1", 512), ("w2", 512), ("w3", 512), ("rw", 512), ("fw", 512), ("fu", 128), ("qu", 128), ("us", 128), ("u1", 128),
                ("u2", 128), ("u3", 128), ("ru", 128), ("qv", 128), ("qe", 512), ("qo", 256), ("qf", C), ("qh", 320),
                ("qn", 136), ("qm", C), ("qx", C)):
     SCRATCH[_n + "c"] = ("sbuf", [128, _w], X4)
@@ -28,9 +32,9 @@ for _n, _w in (("wl", 512), ("w1", 512), ("w2", 512), ("w3", 512), ("rw", 512), 
 for _n, _w in (("xin", 4 * C), ("uin", 512), ("vin", 512), ("ft", 4 * C), ("ht", 4 * C), ("et", 2048), ("ot", 1024),
                ("nt", 544), ("mt", 4 * C), ("zt", 576), ("sg", C), ("thr", C), ("st", 4 * C)):
     SCRATCH[_n] = ("sbuf", [128, _w], "bfloat16")
-for _n in ("iot", "ca", "cb", "cc", "cd", "era", "erb", "ei", "wr", "d16", "d4", "order", "mr", "cr"):
+for _n in ("iot", "ca", "cb", "cc", "cd", "era", "erb", "ei", "wr", "d16", "d4", "order", "mr", "cr", "ma"):
     SCRATCH[_n] = ("sbuf", [128, C], "bfloat16")
-for _n in ("sc2", "sc3", "sc4"):
+for _n in ("sc2", "sc3", "sc4", "sc5"):
     SCRATCH[_n] = ("sbuf", [128, C], "float16")
 for _n in ("tab", "lx", "lt", "ly"):
     SCRATCH[_n] = ("sbuf", [128, 176], "float16")
@@ -41,7 +45,7 @@ for _n, _w in (("mod", 4 * C), ("sc", C), ("psm", 144), ("ea", C), ("opr", C), (
     SCRATCH[_n] = ("sbuf", [128, _w], "float32")
 for _n, _w in (("pt", 176), ("pi", 8), ("pj", 8), ("pk", 8)):
     SCRATCH[_n] = ("sbuf", [128, _w], "int32")
-for _n, _w in (("ls", 176), ("e16", 18), ("w16", 18), ("r16", 18), ("h16", 18), ("c4", 72), ("ul", 8),
+for _n, _w in (("ls", 176), ("e16", 18), ("w16", 18), ("b16", 18), ("r16", 18), ("h16", 18), ("c4", 72), ("ul", 8),
                ("ml", 18), ("ix", 12), ("k16", 18), ("a16", 18)):
     SCRATCH[_n] = ("sbuf", [128, _w], "uint16")
 
@@ -177,19 +181,23 @@ def emit(g, T, ops):
 RELAYED = [[("w", "s", 0, 512), ("w", "c", 0, 256)], [("w", "c", 256, 512), ("u", "c", 0, 128), ("u", "s", 0, 128)]]
 
 
-def relay_program(g, core, src, far, which, T, topo):
+def door_of(dst, src, i, topo):
+    return [c for c in range(WORLD) if topo.mates(c, dst) and topo.die(c) == topo.die(src) and topo.may_write(c, dst)][i]
+
+
+def hand_on(g, core, src, pre, legs, which, T, topo):
     n = count(topo.mask(src, core))
     total = 0
-    for i in range(2):
-        rid, pid = topo.addr(far[i], core)
-        m = topo.mask(core, far[i])
+    for i, (dst, form, sem) in enumerate(legs):
+        rid, pid = topo.addr(dst, core)
+        m = topo.mask(core, dst)
         for k, (name, kind, a, b) in enumerate(RELAYED[which]):
             if i == 0:
                 g.wait_ge(T.sem["ar%d" % k], n)
-            out, in_ = T["%s%d%s" % (name, i + 2, kind)][:, a:b], T["r" + name + kind][:, a:b]
+            out, in_ = T[form % name + kind][:, a:b], T[pre + name + kind][:, a:b]
             if kind == "c":
                 out, in_ = out.bitcast(dt.uint8), in_.bitcast(dt.uint8)
-            g.remote_dma(out, in_, T.sem["aw%d" % (i + 2)], T.sem.sent, pid, rid, m)
+            g.remote_dma(out, in_, T.sem[sem or "ar%d" % k], T.sem.sent, pid, rid, m)
             total += count(m)
     g.wait_ge(T.sem.sent, total)
 
@@ -201,8 +209,14 @@ def rank_program(g, core, T, topo):
         for r, c in enumerate(cores):
             far = [cores[r ^ h] for h in TURN[1:]]
             for which, d in enumerate(relays_of(c, far, T, topo)):
+                straight = [(far[i], "%s" + str(i + 2), "aw%d" % (i + 2)) for i in range(2)]
+                door = door_of(far[1 - which], d, 1 - which, topo)
                 if d == core:
-                    relay_program(g, core, c, far, which, T, topo)
+                    legs = list(straight)
+                    legs[1 - which] = (door, "f%s", None)
+                    hand_on(g, core, c, "r", legs, which, T, topo)
+                if door == core:
+                    hand_on(g, core, d, "f", [straight[1 - which]], which, T, topo)
         return
 
     ops = []
@@ -399,6 +413,7 @@ def rank_program(g, core, T, topo):
             send(["uss"], to[1], T.rus[:], T.uss[:], T.sem.ar2, 9000.0)]
     for i in (1, 2):
         src = relays_of(helpers[i], [cores[rank ^ TURN[i] ^ h] for h in TURN[1:]], T, topo)
+        src[2 - i] = door_of(core, src[2 - i], i - 1, topo)
         arrive(["w%d" % (i + 1), "u%d" % (i + 1)], T.sem["aw%d" % (i + 1)],
                sum(len(RELAYED[k]) * count(topo.mask(src[k], core)) for k in range(2)), like)
     dma("g", ["usc", "uss"], ["vin"], T.vin[:], T.v[:], 9000.0)
@@ -447,8 +462,10 @@ def rank_program(g, core, T, topo):
         wkeys = [["w1s", "w1a"], ["w1s", "w1a"], ["w1s", "w1b"], ["w1s", "w1b"]] if rnd == 0 else [[wn]] * 4
         data_gather("xin" if rnd == 0 else "st", None if rnd == 0 else 0.5, rnd)
         wrap16(e_now, "e16", "sc3")
-        if rnd < 2:
+        if rnd < 2 or LAST:
             scatter("iot", "e16", "ei")
+        if rnd == 2 and LAST:
+            wrap16("ei", "w16", "sc2")
         for i, (a, b) in enumerate(parts):
             quant(ft(a, b), "qf", a, b, T.ft[:, 4 * a:4 * b], ["qf%d" % i])
             for k in range(4):
@@ -487,15 +504,24 @@ def rank_program(g, core, T, topo):
                 lists("", 0, 176)
             tt(["wa", "kk"], ["wb"], T.wb[:], T.wa[:], T.kk[:], A.add)
             src = "ei"
-            for s in range(8):
+            for s in range(NC):
                 dst = ("ca", "cb")[s % 2]
-                gather("s", src, "ls", dst, 0, 18 * s, r=["lsb"] if 18 * s + 18 > 64 else [])
+                gather("s", src, "ls", dst, 0, 18 * s, r=["lsb"])
                 src = dst
-            for i, (a, b) in enumerate(tails):
-                part_gather("s", [src], src, ["ls", "lsb"], "ls", 18 * 8, "wr", i, a, b)
-                part_scan("wr", "d16", "sc2", i, a, b)
-                ts(["sc2%d" % i], ["w16%d" % i], T.w16[:, a // 16:b // 16], T.sc2[:, a + 15:b:16], C + MID, A.add)
-            gather("s", e_now, "w16", e_new, r=["w16%d" % i for i in range(len(tails))])
+            low = "iot"
+            for s in range(NC, 9):
+                dst = ("cc", "cd")[s % 2]
+                gather("s", low, "ls", dst, 0, 18 * s, r=["lsb"])
+                low = dst
+            wrap16(low, "b16", "sc5")
+            if FOLD:
+                wrap16(src, "w16", "sc2")
+                gather("s", e_now, "w16", "wr")
+                gather("s", "wr", "b16", e_new)
+            else:
+                gather("s", src, "b16", "wr")
+                wrap16("wr", "w16", "sc2")
+                gather("s", e_now, "w16", e_new)
             e_now, e_new = e_new, e_now
         else:
             iota(["mod"], T.mod[:], [[0, 4], [1, C]], 0, 0, 4 * C)
@@ -517,11 +543,17 @@ def rank_program(g, core, T, topo):
         tt(["order"], ["psm"], T.psm[:], T.order[:, 0:C:2], T.order[:, 1:C:2], A.add, 300)
         tt(["psm", "h16", "iot"], ["mr"], T.mr[:], T.psm[:].indirect(T.h16[:]), T.iot[:, 0:C], A.subtract, 400)
         if rnd == 2:
-            scatter("mr", "e16", "cr")
+            if LAST:
+                gather("v", "mr", "w16", "cr")
+            else:
+                scatter("mr", "e16", "cr")
             ops[-1]["w"] = ["cr"] + ["cr%d" % i for i in range(len(tails))]
         for i, (a, b) in enumerate(tails):
-            if rnd < 2:
-                part_gather(CR[i], ["mr"], "mr", ["w16%d" % i], "w16", 0, "cr", i, a, b)
+            if rnd < 2 and FOLD:
+                gather(CR[0], "mr", "w16", "ma")
+                part_gather(CR[1], ["ma"], "ma", ["b16"], "b16", 0, "cr", i, a, b)
+            elif rnd < 2:
+                part_gather(CR[0], ["mr"], "mr", ["w16"], "w16", 0, "cr", i, a, b)
             part_wrap4("cr", i, a, b)
 
     data_gather("st", 0.5, 3)
@@ -577,5 +609,20 @@ ORDER = [
     316, 314, 315, 276, 277, 329, 327, 328, 330, 331, 310, 304, 305, 303, 313, 311, 312, 318, 319, 320, 317, 321, 332, 333, 322, 324,
     334, 335, 325, 337, 336, 338, 339, 340, 326, 341, 342, 343, 345, 344, 346, 351, 352, 347, 348, 349, 361, 353, 359, 354, 360, 357,
     356, 355, 362, 358, 350]
+ORDER = [
+    9, 14, 0, 26, 5, 1, 3, 7, 8, 4, 2, 6, 20, 21, 23, 22, 43, 16, 15, 19, 17, 18, 12, 10, 11, 13, 24, 44, 31, 30, 28, 27, 29, 70, 33,
+    25, 62, 59, 35, 34, 32, 42, 63, 36, 49, 39, 64, 48, 45, 47, 37, 38, 91, 66, 92, 60, 40, 65, 98, 67, 41, 99, 76, 68, 100, 77, 101,
+    55, 102, 72, 50, 71, 74, 93, 94, 95, 96, 97, 103, 78, 79, 51, 80, 86, 85, 84, 73, 56, 69, 61, 104, 52, 82, 75, 83, 53, 108, 105,
+    107, 109, 106, 111, 121, 112, 113, 122, 123, 124, 114, 115, 125, 116, 117, 126, 128, 118, 127, 46, 110, 119, 129, 81, 54, 120,
+    130, 131, 132, 133, 139, 140, 141, 57, 143, 58, 142, 135, 134, 137, 144, 145, 136, 138, 146, 149, 147, 148, 151, 152, 153, 150,
+    180, 155, 178, 156, 161, 157, 179, 158, 177, 159, 160, 181, 182, 183, 184, 185, 162, 167, 163, 168, 164, 165, 166, 169, 186, 187,
+    188, 173, 189, 174, 170, 190, 175, 87, 88, 89, 154, 331, 171, 90, 172, 191, 192, 193, 176, 195, 196, 194, 197, 199, 209, 198,
+    202, 201, 212, 211, 200, 210, 213, 203, 206, 205, 216, 215, 214, 217, 207, 204, 218, 208, 221, 220, 219, 222, 225, 229, 228, 227,
+    230, 231, 232, 233, 224, 223, 234, 226, 268, 267, 243, 265, 244, 249, 245, 266, 246, 247, 239, 238, 236, 235, 237, 241, 240, 242,
+    248, 250, 269, 270, 271, 272, 273, 274, 275, 276, 251, 255, 252, 256, 253, 254, 257, 261, 277, 258, 262, 278, 259, 260, 279, 280,
+    281, 282, 263, 286, 264, 283, 296, 289, 288, 284, 292, 298, 299, 302, 300, 297, 290, 287, 293, 303, 301, 291, 304, 294, 305, 295,
+    308, 307, 306, 309, 310, 315, 317, 314, 316, 323, 322, 324, 285, 336, 335, 338, 337, 339, 311, 312, 321, 313, 325, 326, 327, 328,
+    318, 340, 319, 320, 341, 330, 332, 342, 343, 344, 345, 333, 346, 347, 348, 329, 349, 359, 350, 334, 352, 360, 351, 353, 354, 355,
+    356, 357, 369, 358, 363, 364, 365, 370, 366, 361, 362, 367, 368]
 SOON = {"qe0": 5000.0, "qe1": 5000.0, "qo": 2000.0, "ix": 2000.0, "qh": 1000.0, "mta": 4000.0, "mtb": 4000.0, "nt0": 2000.0,
         "thr": 3000.0, "tiny": 2000.0, "tabp": 2000.0, "d16": 1000.0, "d4": 1000.0}

from concourse.mybir import dt, AluOpType, ActivationFunctionType

C = 288
NB = 96
TURN = [1, 2, 4]
WORLD = 256
MID = 144.0
MAGIC = 12582912.0
TINY = 2.0 ** -110
BATCH = False
LIFT = 3.0 * C - MID
SPLIT = 32
HALVES = True
PIECES = [(0, 32), (32, 72)]
WHO = ["vs", "vs", "vs", "vs"]
CR = "sv"
NC = 5
FOLD = True
LAST = False
TAILS = False
FILL = "sss"
EVAC = ["sssvsssv", "ssssssss", "svsvsvsv"]

X4, U8 = "float8_e4m3fn_x4", "uint8"

SCRATCH = {"ps": ("psum", [128, 4096], "float32")}
for _n, _w in (("wl", 512), ("w1", 512), ("w2", 512), ("w3", 512), ("rw", 512), ("fw", 512), ("fu", 128), ("qu", 128), ("us", 128), ("u1", 128),
               ("u2", 128), ("u3", 128), ("ru", 128), ("qv", 128), ("qe", 512), ("qo", 256), ("qf", C), ("qh", 320),
               ("qn", 136), ("qm", C), ("qx", C)):
    SCRATCH[_n + "c"] = ("sbuf", [128, _w], X4)
    SCRATCH[_n + "s"] = ("sbuf", [128, _w], U8)
for _n, _w in (("xin", 4 * C), ("uin", 512), ("vin", 512), ("ft", 4 * C), ("ht", 4 * C), ("et", 2048), ("ot", 1024),
               ("nt", 544), ("mt", 4 * C), ("zt", 576), ("sg", C), ("thr", C), ("st", 4 * C)):
    SCRATCH[_n] = ("sbuf", [128, _w], "bfloat16")
for _n in ("iot", "ca", "cb", "cc", "cd", "era", "erb", "ei", "wr", "d16", "d4", "order", "mr", "cr", "ma"):
    SCRATCH[_n] = ("sbuf", [128, C], "bfloat16")
for _n in ("sc2", "sc3", "sc4", "sc5"):
    SCRATCH[_n] = ("sbuf", [128, C], "float16")
for _n in ("tab", "lx", "lt", "ly"):
    SCRATCH[_n] = ("sbuf", [128, 176], "float16")
SCRATCH["lq"] = ("sbuf", [128, 176], "bfloat16")
for _n, _w in (("mod", 4 * C), ("sc", C), ("psm", 144), ("ea", C), ("opr", C), ("yt", C), ("idn", 176), ("idm", 176), ("sm", 32), ("sm1", 32), ("sm2", 32), ("sm3", 32), ("last", 32), ("dp", 32),
               ("col", 16), ("tiny", 8), ("kk", 32), ("wa", 32), ("wb", 32), ("scol", 8), ("ia", 16), ("ib", 16),
               ("ic", 16), ("ie", 16), ("acol", 16)):
    SCRATCH[_n] = ("sbuf", [128, _w], "float32")
for _n, _w in (("pt", 176), ("pi", 8), ("pj", 8), ("pk", 8)):
    SCRATCH[_n] = ("sbuf", [128, _w], "int32")
for _n, _w in (("ls", 176), ("e16", 18), ("w16", 18), ("b16", 18), ("r16", 18), ("h16", 18), ("c4", 72), ("ul", 8),
               ("ml", 18), ("ix", 12), ("k16", 18), ("a16", 18)):
    SCRATCH[_n] = ("sbuf", [128, _w], "uint16")

SEMAPHORES = (["qv", "qs", "qt", "qg", "sent", "aw1a", "aw1b", "aw1s", "au1", "aw2", "aw3", "ar0", "ar1", "ar2"]
              + ["d%d" % _k for _k in range(40)])

A = AluOpType
F = ActivationFunctionType
WAKE = 70.0


def relays_of(src, far, T, topo):
    return [c for c in topo.cores_of(src)
            if T.rank_of(c) is None and topo.die(c) == topo.die(src) and all(topo.may_write(c, d) for d in far)][:2]


def count(mask):
    return bin(mask).count("1")


def depend(ops):
    wr, rd, groups = {}, {}, {}
    for i, o in enumerate(ops):
        if o["kind"] == "dma":
            groups.setdefault(o["grp"] or "x%d" % i, []).append(i)
    for name, members in groups.items():
        for j in members:
            ops[j]["grp"] = name
    for i, o in enumerate(ops):
        deps = set()
        for k in o["r"]:
            if k in wr:
                deps.add(wr[k])
            if k.startswith("ps") and k != "psm":
                deps.update(j for j in rd.get(k, []) if ops[j]["q"] != o["q"])
        for k in o["w"]:
            if k in wr:
                deps.add(wr[k])
            deps.update(rd.get(k, []))
        for j in list(deps):
            if ops[j]["kind"] == "dma":
                deps.update(groups[ops[j]["grp"]])
        o["deps"] = sorted(j for j in deps if ops[j]["kind"] != "remote")
        for k in o["r"]:
            rd.setdefault(k, []).append(i)
        for k in o["w"]:
            wr[k] = i
            rd[k] = []
    return groups


def arrange(ops):
    n = len(ops)
    level = [o["lat"] for o in ops]
    after = [o["deps"] + o.get("like", []) for o in ops]
    for i in range(n - 1, -1, -1):
        level[i] += ops[i]["tail"]
        for j in after[i]:
            level[j] = max(level[j], ops[j]["lat"] + WAKE + level[i])
    busy = {q: [] for q in "vstgy"}
    start, end = [0.0] * n, [0.0] * n
    for i in sorted(range(n), key=lambda i: (-level[i], i)):
        o = ops[i]
        t = max([o["at"]] + [end[j] + (1.0 if o["q"] == "t" and ops[j]["q"] == "t" else WAKE) for j in after[i]])
        if o["kind"] != "arrive":
            for a, b in sorted(busy[o["q"]]):
                if t + o["c"] <= a:
                    break
                t = max(t, b)
            busy[o["q"]].append((t, t + o["c"]))
        start[i], end[i] = t, t + o["lat"]
    return sorted(range(n), key=lambda i: (start[i], i))


def emit(g, T, ops):
    eng = {"v": g.vector, "s": g.scalar, "t": g.tensor, "g": g, "y": g.sync}
    groups = depend(ops)
    order = ORDER if len(ORDER) == len(ops) else arrange(ops)
    known = {q: {} for q in eng}
    pos = {q: 0 for q in eng}
    for i in order:
        o = ops[i]
        q = o["q"]
        best = {}
        for j in o["deps"]:
            p = ops[j]
            if p["q"] == "t" and q == "t":
                continue
            a, b = p["id"]
            if known[q].get(a, -1) < b and (a not in best or ops[best[a]]["id"][1] < b):
                best[a] = j
        waits = []
        for j in sorted(best.values(), key=lambda j: -len(ops[j]["clock"])):
            p = ops[j]
            if known[q].get(p["id"][0], -1) >= p["id"][1]:
                continue
            waits.append(j)
            p["need"] = True
            for a, b in list(p["clock"].items()) + [p["id"]]:
                if known[q].get(a, -1) < b:
                    known[q][a] = b
        o["waits"] = waits
        o["clock"] = dict(known[q]) if o["kind"] != "arrive" else {}
        if o["kind"] == "op":
            o["id"] = (q, pos[q])
            pos[q] += 1
        else:
            o["id"] = (o["grp"] or "x%d" % i, 0)
    for n, members in enumerate(groups.values()):
        for j in members:
            ops[j]["sem"], ops[j]["val"] = T.sem["d%d" % n], 16 * len(members)
    cnt = {q: 0 for q in eng}
    for i in order:
        o = ops[i]
        q = o["q"]
        for j in o["waits"]:
            eng[q].wait_ge(ops[j]["sem"], ops[j]["val"])
        if o["kind"] == "arrive":
            continue
        ins = o["fn"](eng[q])
        if o["kind"] == "dma":
            ins.then_inc(o["sem"], 16)
        elif o["kind"] == "op" and o.get("need"):
            cnt[q] += 1
            o["sem"], o["val"] = T.sem["q" + q], cnt[q]
            ins.then_inc(o["sem"], 1)
    for members in groups.values():
        if not any(ops[j].get("need") for j in members):
            o = ops[members[-1]]
            eng[o["q"]].wait_ge(o["sem"], o["val"])


RELAYED = [[("w", "s", 0, 512), ("w", "c", 0, 256)], [("w", "c", 256, 512), ("u", "c", 0, 128), ("u", "s", 0, 128)]]


def door_of(dst, src, i, topo):
    return [c for c in range(WORLD) if topo.mates(c, dst) and topo.die(c) == topo.die(src) and topo.may_write(c, dst)][i]


def hand_on(g, core, src, pre, legs, which, T, topo):
    n = count(topo.mask(src, core))
    total = 0
    for i, (dst, form, sem) in enumerate(legs):
        rid, pid = topo.addr(dst, core)
        m = topo.mask(core, dst)
        for k, (name, kind, a, b) in enumerate(RELAYED[which]):
            if i == 0:
                g.wait_ge(T.sem["ar%d" % k], n)
            out, in_ = T[form % name + kind][:, a:b], T[pre + name + kind][:, a:b]
            if kind == "c":
                out, in_ = out.bitcast(dt.uint8), in_.bitcast(dt.uint8)
            g.remote_dma(out, in_, T.sem[sem or "ar%d" % k], T.sem.sent, pid, rid, m)
            total += count(m)
    g.wait_ge(T.sem.sent, total)


def rank_program(g, core, T, topo):
    rank = T.rank_of(core)
    cores = list(T.cores)
    if rank is None:
        for r, c in enumerate(cores):
            far = [cores[r ^ h] for h in TURN[1:]]
            for which, d in enumerate(relays_of(c, far, T, topo)):
                straight = [(far[i], "%s" + str(i + 2), "aw%d" % (i + 2)) for i in range(2)]
                door = door_of(far[1 - which], d, 1 - which, topo)
                if d == core:
                    legs = list(straight)
                    legs[1 - which] = (door, "f%s", None)
                    hand_on(g, core, c, "r", legs, which, T, topo)
                if door == core:
                    hand_on(g, core, d, "f", [straight[1 - which]], which, T, topo)
        return

    ops = []

    def op(q, r, w, fn, c, kind="op", grp=None, lat=None, at=0.0, tail=0.0):
        ops.append({"q": q, "r": r, "w": w, "fn": fn, "kind": kind, "grp": grp, "c": c, "lat": lat or c, "at": at, "tail": tail})

    def el(n):
        return 25.0 + max(64.0, n)

    def dma(q, r, w, out, in_, lat, grp=None, at=0.0, **kw):
        op(q, r, w, lambda e: e.dma_start(out, in_, **kw), 60.0, "dma", grp, lat, at)

    def arrive(w, sem, val, like):
        op("g", [], w, None, 1.0, "arrive")
        ops[-1].update(sem=sem, val=val, like=like)

    sent = [0]

    def send(r, dst, out, in_, sem, lat):
        rid, pid = topo.addr(dst, core)
        m = topo.mask(core, dst)
        op("g", r, [], lambda e: e.remote_dma(out, in_, sem, T.sem.sent, pid, rid, m), 150.0 if sent[0] else 1600.0, "remote", lat=lat)
        sent[0] += count(m)
        return len(ops) - 1

    def u8(name, a, b):
        return T[name][:, a:b].bitcast(dt.uint8)

    def bank(b, a=0, n=C, p=128, step=1):
        return T.ps[0:p, 512 * b + a:512 * b + a + n:step]

    def memset(w, ap, v, n=0):
        op("v", [], w, lambda e: e.memset(ap, v), el(n))

    def ts(r, w, out, in0, s1, o0, s2=None, o1=None, n=0):
        if o1 is None:
            op("v", r, w, lambda e: e.tensor_scalar(out, in0, s1, None, o0), el(n))
        else:
            op("v", r, w, lambda e: e.tensor_scalar(out, in0, s1, s2, o0, o1), el(n))

    def tt(r, w, out, in0, in1, o, n=0):
        op("v", r, w, lambda e: e.tensor_tensor(out, in0, in1, o), el(n))

    def cp(r, w, out, in_, n=0):
        op("v", r, w, lambda e: e.tensor_copy(out, in_), el(n))

    def act(r, w, out, in_, func, n=0, **kw):
        op("s", r, w, lambda e: e.activation(out, in_, func, **kw), el(n) + 10.0)

    def move(q, r, w, out, in_, n, scale=None):
        if q == "s":
            if scale is None:
                act(r, w, out, in_, F.Copy, n)
            else:
                act(r, w, out, in_, F.Copy, n, scale=scale)
        elif scale is None:
            cp(r, w, out, in_, n)
        else:
            ts(r, w, out, in_, scale, A.mult, n=n)

    def quant(r, name, a, b, in_, w=None):
        op("v", r, w or [name], lambda e: e.quantize_mx(T[name + "c"][:, a:b], T[name + "s"][:, a:b], in_), 15.0 + 1.1 * (b - a))

    def mm(r, b, n, l, la, m, ma, start=True, stop=True):
        op("t", r, ["ps%d" % b], lambda e: e.matmul_mx(bank(b, 0, n), T[l + "c"][:, la:la + 128], T[l + "s"][:, la:la + 128],
                                                      T[m + "c"][:, ma:ma + n], T[m + "s"][:, ma:ma + n], start, stop),
           0.63 * (n + 16))

    def gather(q, win, lst, out, a=0, off=0, width=C, r=()):
        move(q, [win, lst] + list(r), [out], T[out][:, 0:C], T[win][:, a:a + width].indirect(T[lst][:, off:off + 18]), 400)

    def scatter(src, lst, out):
        cp([src, lst], [out], T[out][:, 0:C].indirect(T[lst][:]), T[src][:, 0:C], 930)

    def scan(r, src, pat, out, n=150):
        op("v", r + [pat], [out], lambda e: e.tensor_tensor_scan(T[out][:], src, T[pat][:], -2.0 * C, A.max, A.add), el(n))

    def wrap16(row, lst, via):
        scan([row], T[row][:], "d16", via)
        ts([via], [lst], T[lst][:], T[via][:, 15:C:16], C + MID, A.add)

    tails = [(0, 4 * SPLIT), (4 * SPLIT, C)] if TAILS else [(0, C)]

    def part_gather(q, rw, win, rl, lst, off, out, i, a, b):
        move(q, rw + rl, ["%s%d" % (out, i)], T[out][:, a:b], T[win][:].indirect(T[lst][:, off + a // 16:off + b // 16]), 30 + 1.3 * (b - a))

    def part_scan(row, pat, out, i, a, b):
        op("v", ["%s%d" % (row, i), pat], ["%s%d" % (out, i)],
           lambda e: e.tensor_tensor_scan(T[out][:, a:b], T[row][:, a:b], T[pat][:, a:b], -2.0 * C, A.max, A.add), el((b - a) / 2))

    def part_wrap4(row, i, a, b):
        part_scan(row, "d4", "sc4", i, a, b)
        ts(["sc4%d" % i, "col2"], ["c4%d" % i], T.c4[:, a // 4:b // 4], T.sc4[:, a + 3:b:4], 4.0, A.mult, T.col[:, 2:3], A.add)

    def iota(w, out, pattern, base, cm, n, small=True):
        if small:
            op("g", [], w, lambda e: e.iota(out, pattern, base, cm, allow_small_or_imprecise_dtypes=True), 160.0 + 2.1 * n)
        else:
            op("g", [], w, lambda e: e.iota(out, pattern, base, cm), 160.0 + 2.1 * n)

    def select(r, w, out, in_, pattern, cmp, fill, base, cm, n):
        op("g", r, w, lambda e: e.affine_select(out, in_, pattern, cmp, fill, base, cm), 210.0 + 2.1 * n)

    helpers = [cores[rank ^ h] for h in TURN]

    pts = ["pt%d" % s for s in range(8)]
    memset(["pt"], T.pt[:], 0, 176)
    for s in range(8):
        dma("ys"[s % 2], ["pt"], [pts[s]], T.pt[16 * s:128, 18 * s:18 * s + 18], T.p[0:128 - 16 * s, :], 2300.0, "p")
    dma("y", [], ["wls"], T.wls[:], T.ws[:], 2200.0)
    dma("y", [], ["wla"], u8("wlc", 0, 256), T.wc[:, 0:1024], 2900.0, at=600.0)
    dma("y", [], ["wlb"], u8("wlc", 256, 512), T.wc[:, 1024:2048], 3400.0, at=670.0)
    dma("y", [], ["uin"], T.uin[:], T.u[:], 3900.0, at=740.0)
    dma("y", [], ["xin"], T.xin[:], T.x[:], 5000.0, at=810.0)

    iota(["pi"], T.pi[:, 0:1], [[0, 1]], 0, 1, 1, False)
    iota(["sm"], T.sm[:, 0:16], [[1, 16]], 0, 0, 16)
    iota(["smb"], T.sm[:, 16:32], [[0, 4], [1, 4]], 0, 0, 16)
    iota(["idn"], T.idn[:, 0:162], [[0, 9], [16, 18]], 0, 0, 162)
    iota(["iot"], T.iot[:], [[1, C]], -int(MID), 0, C)
    iota(["pk"], T.pk[:, 0:2], [[-112, 2]], 112, 8, 2, False)
    ts(["pi"], ["pj0"], T.pj[:, 0:1], T.pi[:, 0:1], 15, A.bitwise_and)
    ts(["pi"], ["pj1"], T.pj[:, 1:2], T.pi[:, 0:1], 2, A.arith_shift_right, 3, A.bitwise_and)
    ts(["pi"], ["pj2"], T.pj[:, 2:3], T.pi[:, 0:1], 3, A.bitwise_and)
    ts(["pi"], ["pj3"], T.pj[:, 3:4], T.pi[:, 0:1], 4, A.arith_shift_right)
    cp(["pj0", "pj1", "pj2", "pj3"], ["col", "col2"], T.col[:, 0:4], T.pj[:, 0:4])
    ts(["col2"], ["col2"], T.col[:, 2:3], T.col[:, 2:3], 4.0 * (C + MID), A.add)
    memset(["last"], T.last[:], 0.0)
    memset(["last"], T.last[:, 15:32:4], -2.0 * C)
    ts(["col", "idn"], ["idn"], T.idn[:, 0:162], T.idn[:, 0:162], T.col[:, 0:1], A.add, LIFT, A.add, n=162)
    select(["idn"], ["idm"], T.idm[:, 0:162], T.idn[:, 0:162], [[16, 9], [0, 18]], A.is_ge, LIFT, -1, -1, 162)
    ts(["col", "sm"], ["sm1a"], T.sm1[:, 0:16], T.sm[:, 0:16], T.col[:, 0:1], A.subtract)
    ts(["col", "smb"], ["sm1b"], T.sm1[:, 16:32], T.sm[:, 16:32], T.col[:, 1:2], A.subtract)
    ts(["col", "idn"], ["ml"], T.ml[:], T.idn[:, 0:18], 0.0, A.mult, T.col[:, 0:1], A.add)
    ts(["sm1a", "sm1b"], ["sm2"], T.sm2[:], T.sm1[:], 0.0, A.is_equal, float(C), A.mult)
    ts(["sm1a", "sm1b"], ["sm3"], T.sm3[:], T.sm1[:], -1.0, A.is_equal, -1024.0, A.mult)
    tt(["sm2", "last"], ["sm2"], T.sm2[:], T.sm2[:], T.last[:], A.add)
    tt(["sm2", "sm3"], ["dp"], T.dp[:], T.sm2[:], T.sm3[:], A.add)
    gather("s", "dp", "ml", "d16", 0, 0, 16)
    gather("s", "dp", "ml", "d4", 16, 0, 16)
    memset(["ul0"], T.ul[:, 0:6], 0)
    ts(["pk"], ["pk"], T.pk[:, 0:2], T.pk[:, 0:2], 127, A.bitwise_and)
    ts(["pk"], ["ul1"], T.ul[:, 6:8], T.pk[:, 0:2], 1.0, A.add)
    ts(["last"], ["tabp"], T.tab[:, 162:176], T.last[:, 0:14], LIFT, A.add)
    memset(["zt"], T.zt[:], 0.0, 290)
    memset(["ota"], T.ot[:, 0:512], 0.5, 260)
    act(["ota"], ["otb"], T.ot[:, 512:1024], T.ot[:, 0:512], F.Copy, 520, scale=-1.0)
    for how, w, out, in_ in zip(FILL, (["mta"], ["mtb"], ["nt0", "nt1", "nt2"]), (T.mt[:, 0:576], T.mt[:, 576:1152], T.nt[:]),
                                (T.zt[:], T.zt[:], T.zt[:, 0:544])):
        if how == "s":
            act(["zt"], w, out, in_, F.Copy, 590)
        elif how == "v":
            memset(w, out, 0.0, 290)
        else:
            dma("y", ["zt"], w, out, in_, 3000.0)
    memset(["tiny"], T.tiny[:], -TINY)
    for b in range(4):
        select(["ota"], ["et%d" % b], T.et[:, 512 * b:512 * b + 512], T.ot[:, 0:512], [[1, 512]], A.is_equal, 0.0, -b, -4, 512)
    select(["ota"], ["thr"], T.thr[:], T.ot[:, 0:C], [[0, 3], [-1, NB]], A.is_ge, -0.5, 0, 1, C)
    quant(["zt"], "qh", 192, 320, T.zt[:, 0:512])
    quant(["ota", "otb"], "qo", 0, 256, T.ot[:])
    quant(["et0", "et1"], "qe", 0, 256, T.et[:, 0:1024], ["qe0"])
    quant(["et2", "et3"], "qe", 256, 512, T.et[:, 1024:2048], ["qe1"])
    memset(["kk"], T.kk[:], 0.0)
    memset(["kk"], T.kk[:, 16:24], 144.0)
    memset(["kk"], T.kk[:, 8:9], 144.0)
    ts(["idn"], ["ia"], T.ia[:, 0:12], T.idn[:, 0:12], -8.5 - LIFT, A.add, 1.0 / 18.0, A.mult)
    ts(["ia"], ["ia"], T.ia[:, 0:12], T.ia[:, 0:12], MAGIC, A.add, MAGIC, A.subtract)
    ts(["ia", "col"], ["ib"], T.ib[:, 0:12], T.ia[:, 0:12], T.col[:, 3:4], A.subtract, 2.0, A.min)
    ts(["ia"], ["ic"], T.ic[:, 0:12], T.ia[:, 0:12], 0.0, A.is_equal, 7.0, A.mult)
    ts(["ib"], ["ie"], T.ie[:, 0:12], T.ib[:, 0:12], 2.0, A.is_equal, -7.0, A.mult)
    tt(["ic", "ib"], ["ic"], T.ic[:, 0:12], T.ic[:, 0:12], T.ib[:, 0:12], A.subtract)
    tt(["ic", "ie"], ["ic"], T.ic[:, 0:12], T.ic[:, 0:12], T.ie[:, 0:12], A.add)
    ts(["ic"], ["ix"], T.ix[:], T.ic[:, 0:12], 9.0, A.add)
    for o in ops:
        if o["w"] and o["w"][0] in SOON:
            o["tail"] = SOON[o["w"][0]]

    n1 = count(topo.mask(helpers[0], core))
    arrive(["w1s"], T.sem.aw1s, n1, [send(["wls"], helpers[0], T.w1s[:], T.wls[:], T.sem.aw1s, 4200.0)])
    arrive(["w1a"], T.sem.aw1a, n1, [send(["wla"], helpers[0], u8("w1c", 0, 256), u8("wlc", 0, 256), T.sem.aw1a, 3400.0)])
    arrive(["w1b"], T.sem.aw1b, n1, [send(["wlb"], helpers[0], u8("w1c", 256, 512), u8("wlc", 256, 512), T.sem.aw1b, 3800.0)])
    quant(["uin"], "qu", 0, 128, T.uin[:])
    cp(["qu", "ul0", "ul1"], ["usc"], T.usc[:].bitcast(dt.uint32), T.quc[:].bitcast(dt.uint32).indirect(T.ul[:]), 200)
    act(["qu", "ul0", "ul1"], ["uss"], T.uss[:], T.qus[:].indirect(T.ul[:]), F.Copy, 200)
    arrive(["u1"], T.sem.au1, 2 * n1, [send(["usc"], helpers[0], u8("u1c", 0, 128), u8("usc", 0, 128), T.sem.au1, 3500.0),
                                       send(["uss"], helpers[0], T.u1s[:], T.uss[:], T.sem.au1, 3500.0)])
    to = relays_of(core, helpers[1:], T, topo)
    like = [send(["wls", "wlb"], to[0], T.rws[:], T.wls[:], T.sem.ar0, 9000.0),
            send(["wla", "wlb"], to[0], u8("rwc", 0, 256), u8("wlc", 0, 256), T.sem.ar1, 9000.0),
            send(["wlb"], to[1], u8("rwc", 256, 512), u8("wlc", 256, 512), T.sem.ar0, 9000.0),
            send(["usc"], to[1], u8("ruc", 0, 128), u8("usc", 0, 128), T.sem.ar1, 9000.0),
            send(["uss"], to[1], T.rus[:], T.uss[:], T.sem.ar2, 9000.0)]
    for i in (1, 2):
        src = relays_of(helpers[i], [cores[rank ^ TURN[i] ^ h] for h in TURN[1:]], T, topo)
        src[2 - i] = door_of(core, src[2 - i], i - 1, topo)
        arrive(["w%d" % (i + 1), "u%d" % (i + 1)], T.sem["aw%d" % (i + 1)],
               sum(len(RELAYED[k]) * count(topo.mask(src[k], core)) for k in range(2)), like)
    dma("g", ["usc", "uss"], ["vin"], T.vin[:], T.v[:], 9000.0)
    ops[-1]["tail"] = 22000.0
    quant(["vin"], "qv", 0, 128, T.vin[:])

    tt(pts + ["idm"], ["tab"], T.tab[:, 0:162], T.pt[:, 0:162], T.idm[:, 0:162], A.add, 330)
    ts(["tab"], ["ls", "lsb"], T.ls[:, 0:162], T.tab[:, 0:162], LIFT, A.subtract, n=162)
    for s in range(NA):
        gather("s", "iot" if s == 0 else ("cb", "ca")[s % 2], "ls", ("ca", "cb")[s % 2], 0, 18 * s, r=["lsb"])
    for s in range(8 - NA):
        gather("v", "iot" if s == 0 else ("cd", "cc")[s % 2], "ls", ("cc", "cd")[s % 2], 0, 18 * (s + NA), r=["lsb"])
    wrap16(("cc", "cd")[(7 - NA) % 2], "w16", "sc2")
    gather("s", ("ca", "cb")[(NA - 1) % 2], "w16", "era")
    ops[-1]["w"] = ["era", "era0", "era1"]
    ops[-1]["r"] = ops[-1]["r"] + ["w160", "w161"]
    for i, (a, b) in enumerate(tails):
        part_wrap4("era", i, a, b)

    def data_gather(win, scale, turn):
        for i, (a, b) in enumerate(PIECES):
            q = WHO[turn][i]
            move(q, ["c4%d" % k for k, (c, d) in enumerate(tails) if c < 4 * b and d > 4 * a] + [win], ["ft%d" % i], T.ft[:, 16 * a:16 * b], T[win][:].indirect(T.c4[:, a:b]), 30 + 21 * (b - a), scale)

    def ft(a, b):
        return ["ft%d" % i for i, (c, d) in enumerate(PIECES) if 4 * c < b and 4 * d > a]

    def lists(k, a, b):
        n = b - a
        tt(["wa", "ix", "tab", "tabp"], ["lx" + k], T.lx[:, a:b], T.wa[:].indirect(T.ix[:, a // 16:b // 16]), T.tab[:, a:b], A.add, 30 + 1.3 * n)
        ts(["lx" + k], ["lq" + k], T.lq[:, a:b], T.lx[:, a:b], 1.0 / C, A.mult, 128.0 + 0.5 / C, A.add, n=n / 2)
        ts(["lq" + k], ["lt" + k], T.lt[:, a:b], T.lq[:, a:b], 128.0, A.subtract, -float(C), A.mult, n=n / 2)
        op("v", ["lx" + k, "lt" + k], ["ly" + k],
           lambda e: e.tensor_tensor_scan(T.ly[:, a:b], T.lx[:, a:b], T.lt[:, a:b], 0.0, A.max, A.add), el(n / 2))
        ts(["ly" + k], ["ls", "lsb"] if n == 176 else ["ls" + k], T.ls[:, a:b], T.ly[:, a:b], MID, A.add, n=n / 2)

    def compare(key, t, a, b, o):
        ts(["ps7", "scol", "mta", "mtb"], [key], T.mt[0:NB, 4 * a + t:4 * b:4], bank(7, a, b - a, NB), T.scol[0:NB, t:t + 1], o, n=b - a)

    sts = ["st0", "st1", "st2", "st3"]
    e_now, e_new = "era", "erb"
    parts = [(0, 4 * SPLIT), (4 * SPLIT, C)] if HALVES else [(0, C)]
    qh = ["qh%d" % i for i in range(len(parts))]
    for rnd in range(3):
        wn, un = "w%d" % (rnd + 1), "u%d" % (rnd + 1)
        wkeys = [["w1s", "w1a"], ["w1s", "w1a"], ["w1s", "w1b"], ["w1s", "w1b"]] if rnd == 0 else [[wn]] * 4
        data_gather("xin" if rnd == 0 else "st", None if rnd == 0 else 0.5, rnd)
        wrap16(e_now, "e16", "sc3")
        if rnd < 2 or LAST:
            scatter("iot", "e16", "ei")
        if rnd == 2 and LAST:
            wrap16("ei", "w16", "sc2")
        for i, (a, b) in enumerate(parts):
            quant(ft(a, b), "qf", a, b, T.ft[:, 4 * a:4 * b], ["qf%d" % i])
            for k in range(4):
                mm(["qf%d" % i] + wkeys[k], 4 * i + k, b - a, wn, 128 * k, "qf", a)
            for k in range(4):
                move(EVAC[rnd][4 * i + k], ["ps%d" % (4 * i + k)], ["ht%d" % (4 * i + k)], T.ht[:, 4 * a + k:4 * b:4],
                     bank(4 * i + k, 0, b - a), b - a, 0.0078125)
            quant(["ht%d" % (4 * i + k) for k in range(4)] + ["qh"], "qh", a, b, T.ht[:, 4 * a:4 * b], ["qh%d" % i])
        for t in range(3):
            mm([k for k, (a, b) in zip(qh, parts) if a < NB * t + 128 and b > NB * t] + [un], 4 + t, 128, "qh", NB * t, un, 0)
        mm(qh + [un], 7, C, un, 0, "qh", 0)
        mm(qh + [un], 0, C, un, 0, "qh", 0)
        for b in range(3):
            mm(qh + ["qe%d" % (b // 2)], 1 + b, C, "qe", 128 * b, "qh", 0)
        for t in range(3):
            act(["ps%d" % (4 + t), "tiny"], ["nt%d" % t], T.nt[0:NB, 36 + t:96 + t:4], bank(4 + t, 98, 30, NB, 2), F.Sign,
                bias=T.tiny[0:NB, 0:1])
        act(["ps4", "ps5", "ps6"], ["scol"], T.scol[0:NB, 0:3], T.ps[0:NB, 2048:3073:512], F.Copy)
        quant(["nt0", "nt1", "nt2"], "qn", 0, 136, T.nt[:])
        mm(["qn", "qo"], 5, 128, "qo", 0, "qn", 8, True, False)
        mm(["qn", "qo"], 5, 128, "qo", 128, "qn", 0, False, True)
        mm(qh + ["qe1"], 4, C, "qe", 384, "qh", 0)
        for t in range(3):
            act(["ps0", "scol"], ["sg%d" % t], T.sg[0:NB, NB * t:NB * t + NB], bank(0, NB * t, NB, NB), F.Sign, NB,
                bias=T.scol[0:NB, t:t + 1], scale=-1.0)
        for b in range(4):
            act(["ps%d" % (1 + b)] + ft(0, C), [sts[b]], T.st[:, b:4 * C:4], bank(1 + b), F.Copy, 300, scale=2.0)
        dma("g", sts + ft(0, C), ["st"], T.st[:], T.ft[:], 4000.0, accum_op=A.add)
        base = "kk" if rnd == 0 else "wb"
        tt(["ps5", base], ["wa"], T.wa[:], bank(5, 0, 32), T[base][:], A.add)
        if rnd < 2:
            if BATCH:
                lists("", 0, 64)
                lists("b", 64, 176)
            else:
                lists("", 0, 176)
            tt(["wa", "kk"], ["wb"], T.wb[:], T.wa[:], T.kk[:], A.add)
            src = "ei"
            for s in range(NC):
                dst = ("ca", "cb")[s % 2]
                gather("s", src, "ls", dst, 0, 18 * s, r=["lsb"])
                src = dst
            low = "iot"
            for s in range(NC, 9):
                dst = ("cc", "cd")[s % 2]
                gather("s", low, "ls", dst, 0, 18 * s, r=["lsb"])
                low = dst
            wrap16(low, "b16", "sc5")
            if FOLD:
                wrap16(src, "w16", "sc2")
                gather("s", e_now, "w16", "wr")
                gather("s", "wr", "b16", e_new)
            else:
                gather("s", src, "b16", "wr")
                wrap16("wr", "w16", "sc2")
                gather("s", e_now, "w16", e_new)
            e_now, e_new = e_new, e_now
        else:
            iota(["mod"], T.mod[:], [[0, 4], [1, C]], 0, 0, 4 * C)
            ops[-1]["r"] = ["thr", "et3", "usc"]
            cp(["wa", "ix"], ["acol"], T.acol[:], T.wa[:].indirect(T.ix[:, 0:1]))
            ts(["acol", "e16"], ["a16"], T.a16[:], T.e16[:], T.acol[:, 0:1], A.subtract, 3.0 * C, A.add)
            gather("s", "mod", "a16", "ea", 0, 0, 4 * C)
        compare("mt0", 0, NB, C, A.is_le)
        compare("mt1", 1, 0, NB, A.is_lt)
        compare("mt2", 1, 2 * NB, C, A.is_le)
        compare("mt3", 2, 0, 2 * NB, A.is_lt)
        tt(["sg0", "sg1", "sg2", "thr", "mta", "mtb"], ["mt4"], T.mt[0:NB, 3:4 * C:4], T.sg[0:NB, :], T.thr[0:NB, :], A.is_gt, 590)
        quant(["mt0", "mt1", "mt2", "mt3", "mt4"], "qm", 0, C, T.mt[:])
        mm(["qm", "qo"], 6, C, "qo", 0, "qm", 0)
        scan(["ps6"], bank(6), "d16", "sc", 300)
        ts(["sc"], ["r16"], T.r16[:], T.sc[:, 15:C:16], float(C), A.add, 2.0, A.mult)
        ts(["sc"], ["h16"], T.h16[:], T.sc[:, 15:C:16], C - 0.25, A.add)
        scatter("iot", "r16", "order")
        tt(["order"], ["psm"], T.psm[:], T.order[:, 0:C:2], T.order[:, 1:C:2], A.add, 300)
        tt(["psm", "h16", "iot"], ["mr"], T.mr[:], T.psm[:].indirect(T.h16[:]), T.iot[:, 0:C], A.subtract, 400)
        if rnd == 2:
            if LAST:
                gather("v", "mr", "w16", "cr")
            else:
                scatter("mr", "e16", "cr")
            ops[-1]["w"] = ["cr"] + ["cr%d" % i for i in range(len(tails))]
        for i, (a, b) in enumerate(tails):
            if rnd < 2 and FOLD:
                gather(CR[0], "mr", "w16", "ma")
                part_gather(CR[1], ["ma"], "ma", ["b16"], "b16", 0, "cr", i, a, b)
            elif rnd < 2:
                part_gather(CR[0], ["mr"], "mr", ["w16"], "w16", 0, "cr", i, a, b)
            part_wrap4("cr", i, a, b)

    data_gather("st", 0.5, 3)
    a = 4 * SPLIT
    quant(ft(0, a), "qx", 0, a, T.ft[:, 0:4 * a], ["qxa"])
    quant(ft(a, C), "qx", a, C, T.ft[:, 4 * a:4 * C], ["qxb"])
    mm(["qxa", "qv"], 0, a, "qv", 0, "qx", 0)
    mm(["qxb", "qv"], 7, C - a, "qv", 0, "qx", a)
    dma("y", ["qxa"], [], T.oc[:, 0:4 * a], u8("qxc", 0, a), 2300.0, "o")
    dma("y", ["qxb"], [], T.oc[:, 4 * a:4 * C], u8("qxc", a, C), 2300.0, "o")
    wrap16("cr", "k16", "sc3")
    move("s", ["ps0"], ["yta"], T.yt[:, 0:a], bank(0, 0, a), a)
    move("s", ["ps7"], ["ytb"], T.yt[:, a:C], bank(7, 0, C - a), C - a)
    for k in range(4):
        dma("y", ["qxa", "qxb"], [], T.osc[4 * k:4 * k + 4, :], T.qxs[32 * k:32 * k + 4, :], 2000.0, "o")
    dma("s", ["yta"], [], T.y[:, 0:a], T.yt[:, 0:a], 2300.0, "z")
    dma("s", ["ytb"], [], T.y[:, a:C], T.yt[:, a:C], 2300.0, "z")
    gather("v", "ea", "k16", "opr")
    dma("y", ["opr"], [], T.op[:], T.opr[0:128:16, :], 2000.0, "o")

    emit(g, T, ops)
    g.wait_ge(T.sem.sent, sent[0])


NA = 5
ORDER = [
    15, 14, 19, 16, 17, 18, 0, 44, 22, 23, 21, 43, 20, 9, 4, 8, 6, 2, 5, 7, 3, 1, 11, 10, 12, 13, 59, 24, 26, 28, 31, 30, 27, 62, 33,
    34, 60, 32, 35, 63, 36, 29, 70, 74, 50, 72, 84, 71, 45, 48, 64, 65, 66, 91, 61, 92, 37, 38, 67, 25, 49, 98, 39, 40, 99, 68, 100,
    55, 101, 76, 102, 41, 93, 94, 95, 96, 97, 103, 78, 56, 77, 104, 105, 107, 47, 75, 51, 79, 80, 73, 86, 82, 85, 83, 53, 81, 52, 89,
    54, 108, 106, 109, 111, 121, 110, 115, 114, 112, 124, 125, 122, 123, 113, 118, 116, 128, 126, 127, 117, 129, 119, 130, 120, 57,
    42, 69, 46, 133, 132, 131, 141, 140, 139, 142, 143, 58, 136, 135, 144, 145, 137, 138, 146, 134, 150, 147, 149, 148, 151, 153,
    152, 155, 156, 157, 158, 159, 160, 176, 175, 174, 177, 178, 162, 163, 164, 165, 166, 167, 168, 169, 170, 179, 161, 90, 180, 181,
    182, 183, 184, 185, 186, 171, 172, 187, 188, 173, 154, 189, 192, 190, 195, 191, 193, 205, 323, 87, 194, 196, 199, 208, 207, 209,
    197, 206, 198, 200, 203, 212, 211, 213, 210, 202, 201, 214, 204, 217, 216, 215, 225, 224, 223, 226, 227, 220, 218, 222, 228, 229,
    219, 230, 221, 234, 236, 231, 233, 232, 237, 235, 261, 259, 88, 238, 239, 240, 241, 242, 243, 244, 260, 258, 262, 246, 247, 248,
    249, 250, 251, 252, 253, 254, 263, 264, 245, 265, 266, 267, 268, 269, 270, 255, 256, 271, 272, 273, 274, 278, 257, 275, 288, 282,
    281, 280, 289, 292, 279, 290, 291, 286, 284, 296, 285, 294, 293, 283, 287, 295, 297, 276, 298, 300, 299, 301, 302, 306, 309, 307,
    308, 314, 315, 316, 277, 328, 330, 327, 329, 331, 310, 305, 303, 304, 313, 311, 312, 319, 317, 320, 318, 321, 332, 333, 322, 324,
    334, 325, 335, 336, 337, 338, 339, 340, 326, 341, 342, 344, 343, 345, 346, 351, 352, 347, 348, 349, 361, 353, 359, 354, 360, 355,
    357, 358, 362, 356, 350]
ORDER = [
    14, 19, 16, 15, 17, 18, 0, 43, 23, 20, 22, 21, 9, 2, 8, 6, 4, 5, 3, 1, 7, 10, 12, 11, 13, 26, 24, 44, 27, 28, 31, 30, 62, 33, 32,
    25, 35, 34, 63, 40, 36, 64, 29, 39, 66, 41, 91, 59, 70, 72, 51, 74, 84, 71, 47, 48, 45, 37, 38, 92, 65, 98, 49, 67, 93, 94, 95,
    96, 97, 99, 68, 76, 100, 77, 101, 55, 102, 103, 56, 60, 42, 69, 104, 78, 79, 50, 75, 80, 82, 85, 86, 83, 52, 53, 73, 54, 81, 105,
    108, 107, 106, 109, 111, 121, 113, 112, 123, 124, 114, 125, 122, 115, 117, 127, 128, 118, 126, 116, 110, 129, 119, 130, 120, 61,
    57, 46, 133, 132, 131, 141, 140, 139, 142, 143, 58, 135, 136, 144, 145, 137, 138, 134, 146, 147, 149, 148, 150, 151, 152, 153,
    155, 156, 157, 158, 159, 175, 160, 176, 174, 177, 178, 162, 163, 164, 165, 166, 167, 168, 169, 170, 89, 154, 87, 179, 180, 161,
    181, 182, 183, 184, 90, 185, 186, 88, 323, 171, 172, 187, 173, 188, 192, 189, 190, 191, 195, 193, 205, 194, 199, 196, 208, 209,
    197, 206, 207, 198, 203, 200, 212, 213, 210, 211, 201, 202, 214, 204, 217, 215, 216, 225, 223, 224, 226, 220, 218, 222, 227, 228,
    229, 221, 219, 230, 234, 236, 235, 232, 231, 237, 233, 261, 260, 239, 240, 241, 242, 243, 244, 246, 247, 248, 249, 250, 251, 252,
    253, 254, 258, 259, 262, 263, 264, 245, 265, 238, 266, 267, 268, 269, 270, 255, 256, 271, 272, 273, 274, 278, 257, 275, 288, 280,
    281, 282, 284, 289, 290, 286, 294, 279, 292, 296, 291, 285, 293, 283, 295, 287, 297, 298, 299, 300, 301, 302, 306, 307, 309, 308,
    316, 314, 315, 276, 277, 329, 327, 328, 330, 331, 310, 304, 305, 303, 313, 311, 312, 318, 319, 320, 317, 321, 332, 333, 322, 324,
    334, 335, 325, 337, 336, 338, 339, 340, 326, 341, 342, 343, 345, 344, 346, 351, 352, 347, 348, 349, 361, 353, 359, 354, 360, 357,
    356, 355, 362, 358, 350]
ORDER = [
    9, 14, 0, 26, 5, 1, 3, 7, 8, 4, 2, 6, 20, 21, 23, 22, 43, 16, 15, 19, 17, 18, 12, 10, 11, 13, 24, 44, 31, 30, 28, 27, 29, 70, 33,
    25, 62, 59, 35, 34, 32, 42, 63, 36, 49, 39, 64, 48, 45, 47, 37, 38, 91, 66, 92, 60, 40, 65, 98, 67, 41, 99, 76, 68, 100, 77, 101,
    55, 102, 72, 50, 71, 74, 93, 94, 95, 96, 97, 103, 78, 79, 51, 80, 86, 85, 84, 73, 56, 69, 61, 104, 52, 82, 75, 83, 53, 108, 105,
    107, 109, 106, 111, 121, 112, 113, 122, 123, 124, 114, 115, 125, 116, 117, 126, 128, 118, 127, 46, 110, 119, 129, 81, 54, 120,
    130, 131, 132, 133, 139, 140, 141, 57, 143, 58, 142, 135, 134, 137, 144, 145, 136, 138, 146, 149, 147, 148, 151, 152, 153, 150,
    180, 155, 178, 156, 161, 157, 179, 158, 177, 159, 160, 181, 182, 183, 184, 185, 162, 167, 163, 168, 164, 165, 166, 169, 186, 187,
    188, 173, 189, 174, 170, 190, 175, 87, 88, 89, 154, 331, 171, 90, 172, 191, 192, 193, 176, 195, 196, 194, 197, 199, 209, 198,
    202, 201, 212, 211, 200, 210, 213, 203, 206, 205, 216, 215, 214, 217, 207, 204, 218, 208, 221, 220, 219, 222, 225, 229, 228, 227,
    230, 231, 232, 233, 224, 223, 234, 226, 268, 267, 243, 265, 244, 249, 245, 266, 246, 247, 239, 238, 236, 235, 237, 241, 240, 242,
    248, 250, 269, 270, 271, 272, 273, 274, 275, 276, 251, 255, 252, 256, 253, 254, 257, 261, 277, 258, 262, 278, 259, 260, 279, 280,
    281, 282, 263, 286, 264, 283, 296, 289, 288, 284, 292, 298, 299, 302, 300, 297, 290, 287, 293, 303, 301, 291, 304, 294, 305, 295,
    308, 307, 306, 309, 310, 315, 317, 314, 316, 323, 322, 324, 285, 336, 335, 338, 337, 339, 311, 312, 321, 313, 325, 326, 327, 328,
    318, 340, 319, 320, 341, 330, 332, 342, 343, 344, 345, 333, 346, 347, 348, 329, 349, 359, 350, 334, 352, 360, 351, 353, 354, 355,
    356, 357, 369, 358, 363, 364, 365, 370, 366, 361, 362, 367, 368]
SOON = {"qe0": 5000.0, "qe1": 5000.0, "qo": 2000.0, "ix": 2000.0, "qh": 1000.0, "mta": 4000.0, "mtb": 4000.0, "nt0": 2000.0,
        "thr": 3000.0, "tiny": 2000.0, "tabp": 2000.0, "d16": 1000.0, "d4": 1000.0}
